import numpy as np, ml_dtypes
CORES = [13,21,141,149]
N = 4
BF = ml_dtypes.bfloat16
def gentries(a):
    return np.ascontiguousarray(a.reshape(8, 16, -1).transpose(0, 2, 1)).reshape(8, -1)
def gtable(e):
    e = np.asarray(e); return np.ascontiguousarray(e.reshape(8, -1, 16).transpose(0, 2, 1)).reshape(128, -1).astype(np.int32)
H, W, P = 64, 64, 4096
A, B, Q = 16, 32, 512
SW = 2
def pack(F, U, S, J):
    return {"fr": np.ascontiguousarray(F).reshape(N, 128, P).astype(np.float32).astype(BF), "qu": np.ascontiguousarray(U).reshape(N, 128, Q).astype(np.float32).astype(BF),
            "st": np.stack([gtable(v) for v in S]), "ju": np.stack([gtable(v) for v in J])}
def jumps(rng):
    n = (N, 8, SW * Q)
    return np.where(rng.random(n) < 0.5, rng.integers(-2, 3, n) * W + rng.integers(-2, 3, n), rng.integers(1 - P, P, n))
def scene(rng):
    base = rng.integers(0, 16, (8, 16, H, W)); dy = np.add.accumulate(rng.integers(-1, 2, (N, 8)), axis=0); dx = np.add.accumulate(rng.integers(-1, 2, (N, 8)), axis=0)
    F = np.zeros((N, 8, 16, H, W), np.int64); U = np.zeros((N, 8, 16, A, B), np.int64); S = np.zeros((N, 8, Q), np.int64)
    for r in range(N):
        for g in range(8):
            F[r, g] = np.roll(base[g], (int(dy[r, g]), int(dx[r, g])), axis=(1, 2))
            yy = (rng.integers(0, H) + np.arange(A)) % H; xx = (rng.integers(0, W) + np.arange(B)) % W
            U[r, g] = base[g][:, yy][:, :, xx]
            S[r, g] = (((yy + dy[r, g]) % H)[:, None] * W + ((xx + dx[r, g]) % W)[None, :]).reshape(-1)
    F = np.where(rng.random(F.shape) < 0.1, rng.integers(0, 16, F.shape), F); U = np.where(rng.random(U.shape) < 0.2, rng.integers(0, 16, U.shape), U)
    S = np.where(rng.random(S.shape) < 0.1, S, rng.integers(0, P, S.shape))
    return F.reshape(N, 8, 16, P), U.reshape(N, 8, 16, Q), S, jumps(rng)
def setup_inputs(rng):
    return pack(*scene(rng))
def setup_inputs_ties(rng):
    pat = rng.integers(0, 16, (8, 13, 16)); g = np.arange(8)[None, :, None]
    sub = np.argsort(rng.random((N, 8, 12)), axis=-1)[..., :6]
    idx = np.take_along_axis(sub, rng.integers(0, 6, (N, 8, P)), axis=-1)
    F = pat[g, idx].transpose(0, 1, 3, 2); U = pat[g, rng.integers(0, 13, (N, 8, Q))].transpose(0, 1, 3, 2)
    return pack(F, U, rng.integers(0, P, (N, 8, Q)), jumps(rng))
def setup_inputs_edges(rng):
    F, U, S, J = scene(rng)
    S = rng.choice(np.array([0, 1, H - 2, H - 1]), S.shape) * W + rng.choice(np.array([0, 1, W - 2, W - 1]), S.shape)
    J = rng.choice(np.array([0, 1, -1, W, -W, W - 1, P - 1, 1 - P]), J.shape)
    return pack(F, U, S, J)
def setup_inputs_far(rng):
    F = 15 * rng.integers(0, 2, (N, 8, 16, P)); U = 15 * rng.integers(0, 2, (N, 8, 16, Q)); h = rng.integers(0, 8)
    F[:, h] = 15; U[:, h] = 0
    return pack(F, U, rng.integers(0, P, (N, 8, Q)), jumps(rng))
def setup_inputs_one(rng):
    F, U, S, J = scene(rng)
    S = np.zeros_like(S) + rng.integers(0, P, (N, 8, 1)); J = np.zeros_like(J) + rng.integers(1 - P, P, (N, 8, 1))
    J[rng.integers(0, N)] = 0; k = rng.integers(0, N); F[k] = F[k][:, :, :1]
    return pack(F, U, S, J)
def setup_inputs_spread(rng):
    def uneven(n):
        e = np.exp2(rng.integers(-2, 4, (N, 8, 1, n))); v = np.minimum(np.floor(16 * rng.random((N, 8, 16, n)) ** e), 15)
        return v * (rng.random((N, 8, 1, n)) > 0.0625)
    F = uneven(P); U = uneven(Q)
    S = np.minimum(np.floor(P * rng.random((N, 8, Q)) ** 3), P - 1).astype(np.int64); S[:, :, 5] = P - 1
    J = rng.integers(1 - P, P, (N, 8, SW * Q)); J[:, :, 0] = P - 1; J[:, :, 1] = 1 - P
    return pack(F, U, S, J)
def check_inputs(d):
    bad = []
    for nm in ("fr", "qu"):
        v = d[nm].astype(np.float32)
        if not (np.isfinite(v).all() and (v == np.floor(v)).all() and v.min() >= 0 and v.max() <= 15): bad.append(nm)
    if d["st"].min() < 0 or d["st"].max() > P - 1: bad.append("st")
    if d["ju"].min() < 1 - P or d["ju"].max() > P - 1: bad.append("ju")
    return bad
def sides(p, t):
    i = np.arange(Q)
    if t == 1:
        a = np.roll(p, -1, axis=1); b = np.roll(p, -B, axis=1)
        return np.where(i % B < B - 1, a - (a % W > 0), p), np.where(i < Q - B, np.where(b >= W, b - W, b), p)
    a = np.roll(p, 1, axis=1); b = np.roll(p, B, axis=1)
    return np.where(i % B > 0, a + (a % W < W - 1), p), np.where(i >= B, np.where(b + W < P, b + W, b), p)
def reference(fr, qu, st, ju):
    F = fr.astype(np.int32).reshape(N, 8, 16, P); U = qu.astype(np.int32).reshape(N, 8, 16, Q)
    yc = np.zeros((N, 128, Q // 16), np.float32); yf = np.zeros_like(yc); yp = np.zeros_like(yc)
    for r in range(N):
        p = gentries(st[r]).astype(np.int64)
        bc = np.full((8, Q), 1 << 20, np.int64); bf = np.zeros((8, Q), np.int64); bp = np.zeros((8, Q), np.int64)
        for s in range(N):
            k = (r + s) % N; J = gentries(ju[k]).astype(np.int64).reshape(8, SW, Q)
            for t in range(SW):
                one, two = sides(p, t)
                c = np.stack([p, one, two, np.minimum(np.maximum(p + J[:, t], 0), P - 1)], axis=1)
                v = np.take_along_axis(F[k], c.reshape(8, 1, 4 * Q), axis=2).reshape(8, 16, 4, Q) - U[r][:, :, None, :]
                e = np.sum(v * v, axis=1); w = np.argmin(e, axis=1)[:, None]
                p = np.take_along_axis(c, w, axis=1)[:, 0]; best = np.take_along_axis(e, w, axis=1)[:, 0]
            m = best < bc
            bc = np.where(m, best, bc); bf = np.where(m, k, bf); bp = np.where(m, p, bp)
        yc[r] = gtable(bc); yf[r] = gtable(bf); yp[r] = gtable(bp)
    return {"yc": yc, "yf": yf, "yp": yp}

@@ -1,0 +1,567 @@
+import numpy as np
+from concourse.mybir import AluOpType, ActivationFunctionType
+
+NJ = 128
+NF = 4096
+NQ = (NJ + NF) // 4
+BIG = 8192.0
+WMAX = 24
+OPT = {
+    "rows0": 10,
+    "side": [3, 2],
+    "pre": [0.4],
+    "frac": 0.7,
+    "tail": [2],
+    "last": [12, 6, 2],
+    "lastpre": 1,
+}
+
+SCRATCH = {
+    "fb0": ("sbuf", [128, NJ + NF], "bfloat16"),
+    "fb1": ("sbuf", [128, NJ + NF], "bfloat16"),
+    "fb2": ("sbuf", [128, NJ + NF], "bfloat16"),
+    "fb3": ("sbuf", [128, NJ + NF], "bfloat16"),
+    "q": ("sbuf", [128, 512], "bfloat16"),
+    "qrep": ("sbuf", [128, 32, 64], "bfloat16"),
+    "q4": ("sbuf", [128, 32 * 64], "bfloat16"),
+    "q3": ("sbuf", [128, 32 * 48], "bfloat16"),
+    "sqr": ("sbuf", [128, 2 * WMAX, 80], "bfloat16"),
+    "gs": ("sbuf", [128, 256], "bfloat16"),
+    "sti": ("sbuf", [128, 32], "int32"),
+    "jui": ("sbuf", [128, 64], "int32"),
+    "jt": ("sbuf", [128, 128], "int32"),
+    "vv": ("sbuf", [128, 256], "bfloat16"),
+    "pi": ("sbuf", [128, 8], "int32"),
+    "col": ("sbuf", [128, 8], "float32"),
+    "tsel": ("sbuf", [128, 144], "bfloat16"),
+    "mh": ("sbuf", [128, 5 * 128], "float16"),
+    "mb": ("sbuf", [128, 7 * 128], "bfloat16"),
+    "mf": ("sbuf", [128, 128], "float32"),
+    "mask0": ("sbuf", [128, 160], "bfloat16"),
+    "mask1": ("sbuf", [128, 160], "bfloat16"),
+    "mask7": ("sbuf", [128, 32, 8], "bfloat16"),
+    "plc0": ("sbuf", [128, 32, 8], "bfloat16"),
+    "plc1": ("sbuf", [128, 32, 8], "bfloat16"),
+    "floor": ("sbuf", [128, 160], "float32"),
+    "d1": ("sbuf", [128, 160], "float32"),
+    "floor7": ("sbuf", [128, 256], "float32"),
+    "dpf": ("sbuf", [128, 256], "float32"),
+    "cf": ("sbuf", [128, 128], "float32"),
+    "p16": ("sbuf", [128, 8 * 160], "float16"),
+    "z0": ("sbuf", [128, 32], "float32"),
+    "a1": ("sbuf", [128, 8 * 32], "bfloat16"),
+    "na": ("sbuf", [128, 8 * 32], "bfloat16"),
+    "sg": ("sbuf", [128, 8 * 32], "bfloat16"),
+    "oc": ("sbuf", [128, 32], "float32"),
+    "of": ("sbuf", [128, 32], "float32"),
+    "op": ("sbuf", [128, 32], "float32"),
+    "p7": ("psum", [128, 64, 8], "float32"),
+    "pg": ("psum", [128, 512], "float32"),
+}
+for _x in "AB":
+    SCRATCH["d" + _x] = ("sbuf", [128, WMAX * 64], "bfloat16")
+    SCRATCH["lst" + _x] = ("sbuf", [128, WMAX * 4], "uint16")
+    for _n in ("m", "c", "t1", "dp", "ni", "z", "zf"):
+        SCRATCH[_n + _x] = ("sbuf", [128, WMAX * 8 + 8], "float32")
+    SCRATCH["ps" + _x] = ("psum", [128, 512], "float32")
+    SCRATCH["pl" + _x] = ("psum", [128, 64, 8], "float32")
+    SCRATCH["pc" + _x] = ("psum", [128, 512], "float32")
+
+SEMAPHORES = ["sv", "sa", "sp", "sq", "ld0", "ld1", "ld2", "ld3", "lj", "ls", "lq", "sent", "arr",
+              "fj1", "fj2", "fj3", "fa1", "fa2", "fa3", "out0", "out1", "out2"]
+
+
+def relays_of(T, topo, src):
+    others = [d for d in T.cores if d != src]
+    rel = [c for c in topo.cores_of(src) if c != src and all(topo.may_write(c, d) for d in others)]
+    far = [c for c in rel if topo.die(c) != topo.die(src)]
+    near = [c for c in rel if topo.die(c) == topo.die(src)]
+    out = []
+    while far or near:
+        if far:
+            out.append(far.pop(0))
+        if near:
+            out.append(near.pop(0))
+    return out[:4]
+
+
+def nbits(m):
+    return bin(m).count("1")
+
+
+def relay_program(g, core, T, topo, src, k):
+    n = len(T.cores)
+    r = T.rank_of(src)
+    part = T.fb0[:, k * NQ:(k + 1) * NQ]
+    g.wait_ge(T.sem.arr, nbits(topo.mask(src, core)))
+    total = 0
+    for step in range(1, n):
+        d = T.cores[(r - step) % n]
+        rid, pid = topo.addr(d, core)
+        m = topo.mask(core, d)
+        sem = T.sem[("fj%d" if k == 0 else "fa%d") % step]
+        g.remote_dma(T["fb%d" % step][:, k * NQ:(k + 1) * NQ], part, sem, T.sem.sent, pid, rid, m)
+        total += nbits(m)
+    g.wait_ge(T.sem.sent, total)
+
+
+def make_emitter(g, T):
+    queues = {"v": g.vector, "a": g.scalar, "p": g.tensor, "g": g, "s": g.sync}
+    own = {"v": "sv", "a": "sa", "p": "sp", "g": "sq"}
+    count = {"sv": 0, "sa": 0, "sp": 0, "sq": 0}
+    known = {q: {} for q in queues}
+    hist = {}
+    grids = {}
+
+    def ap(name, *idx):
+        if name not in grids:
+            shp = SCRATCH[name][1][1:]
+            grids[name] = np.arange(int(np.prod(shp))).reshape(shp)
+        full = (slice(None),) + tuple(idx)
+        if SCRATCH[name][0] == "psum":
+            bits = 1
+        else:
+            flags = np.zeros(grids[name].size, np.uint8)
+            flags[grids[name][tuple(idx)].reshape(-1) if idx else slice(None)] = 1
+            bits = int.from_bytes(np.packbits(flags, bitorder="little").tobytes(), "little")
+        return (T[name][full], name, bits)
+
+    def wait(q, ev):
+        sem, val, clock = ev
+        if known[q].get(sem, 0) >= val:
+            return
+        queues[q].wait_ge(T.sem[sem], val)
+        known[q][sem] = val
+        for s, v in clock.items():
+            if known[q].get(s, 0) < v:
+                known[q][s] = v
+
+    def note(q, ev, reads, writes):
+        for a in writes:
+            h = hist.setdefault(a[1], [])
+            h[:] = [e for e in h if e[1] & ~a[2]]
+            h.append((ev, a[2], True, q))
+        for a in reads:
+            hist.setdefault(a[1], []).append((ev, a[2], False, q))
+
+    def deps(q, reads, writes):
+        need = []
+        for a in reads:
+            psum = SCRATCH[a[1]][0] == "psum"
+            for e in hist.get(a[1], []):
+                if e[1] & a[2] and (e[2] or (psum and e[3] != q)):
+                    need.append(e[0])
+        for a in writes:
+            psum = SCRATCH[a[1]][0] == "psum"
+            for e in hist.get(a[1], []):
+                if e[1] & a[2] and not (psum and q == "p" and e[3] == "p"):
+                    need.append(e[0])
+        best = {}
+        for ev in need:
+            if ev[0] not in best or best[ev[0]][1] < ev[1]:
+                best[ev[0]] = ev
+        for ev in best.values():
+            wait(q, ev)
+
+    def op(q, fn, reads, writes):
+        deps(q, reads, writes)
+        sem = own[q]
+        count[sem] += 1
+        fn(queues[q]).then_inc(T.sem[sem], 1)
+        ev = (sem, count[sem], dict(known[q]))
+        note(q, ev, reads, writes)
+        return ev
+
+    def dma(q, out, in_, sem, reads, writes):
+        deps(q, reads, writes)
+        queues[q].dma_start(out, in_).then_inc(T.sem[sem], 16)
+        ev = (sem, 16, dict(known[q]))
+        note("dma", ev, reads, writes)
+        return ev
+
+    def landed(a, sem, val):
+        note("dma", (sem, val, {}), [], [a])
+
+    def finish(q, evs):
+        for sem, v in count.items():
+            if v:
+                wait(q, (sem, v, {}))
+        for ev in evs:
+            wait(q, ev)
+
+    return ap, op, dma, landed, deps, finish
+
+
+def rank_body(g, core, T, topo, rank):
+    n = len(T.cores)
+    ALU, ACT = AluOpType, ActivationFunctionType
+    ap, op, dma, landed, deps, finish = make_emitter(g, T)
+    S = slice
+    rows_a = [OPT["rows0"] - (s + 1) // 2 for s in range(8)]
+
+    def ts(out, in0, s1, s2, o0, o1=None):
+        a1 = s1[0] if isinstance(s1, tuple) else s1
+        a2 = s2[0] if isinstance(s2, tuple) else s2
+        rd = [in0] + [s for s in (s1, s2) if isinstance(s, tuple)]
+        if o1 is None:
+            return op("v", lambda e: e.tensor_scalar(out[0], in0[0], a1, None, o0), rd, [out])
+        return op("v", lambda e: e.tensor_scalar(out[0], in0[0], a1, a2, o0, o1), rd, [out])
+
+    def tt(out, in0, in1, o):
+        return op("v", lambda e: e.tensor_tensor(out[0], in0[0], in1[0], o), [in0, in1], [out])
+
+    def cp(out, in0):
+        return op("v", lambda e: e.tensor_copy(out[0], in0[0]), [in0], [out])
+
+    def fill(out, val):
+        return op("v", lambda e: e.memset(out[0], val), [], [out])
+
+    def scan(out, d0, d1, init, o0, o1):
+        return op("v", lambda e: e.tensor_tensor_scan(out[0], d0[0], d1[0], init, o0, o1), [d0, d1], [out])
+
+    def act(out, in0, func, bias=0.0, scale=1.0):
+        b = bias[0] if isinstance(bias, tuple) else bias
+        rd = [in0] + ([bias] if isinstance(bias, tuple) else [])
+        return op("a", lambda e: e.activation(out[0], in0[0], func, bias=b, scale=scale), rd, [out])
+
+    def mm(out, lhs, rhs, start=False, stop=False):
+        return op("p", lambda e: e.matmul(out[0], lhs[0], rhs[0], start, stop), [lhs, rhs], [out])
+
+    def aset(out, cnt, val):
+        act(out, ap("vv", S(0, cnt)), ACT.Identity, bias=val, scale=0.0)
+
+    def gset(out, cnt, val):
+        op("g", lambda e: e.iota(out[0], [[0, cnt]], int(val), 0, allow_small_or_imprecise_dtypes=True), [], [out])
+
+    def pst(s, c0, c1, step=1):
+        return ap("p16", S(160 * s + 5 * c0 + 4, 160 * s + 5 * c1, 5 * step))
+
+    allc = S(0, 32)
+
+    a = ap("jui"); dma("a", a[0], T.ju[:], "lj", [], [a])
+    a = ap("sti"); dma("a", a[0], T.st[:], "ls", [], [a])
+    a = ap("q"); dma("a", a[0], T.qu[:], "lq", [], [a])
+    for k in range(4):
+        lo, hi = max(k * NQ, NJ), (k + 1) * NQ
+        a = ap("fb0", S(lo, hi)); dma("s", a[0], T.fr[:, lo - NJ:hi - NJ], "ld%d" % k, [], [a])
+    for step in range(1, n):
+        src = T.cores[(rank + step) % n]
+        rel = relays_of(T, topo, src)
+        landed(ap("fb%d" % step, S(0, NQ)), "fj%d" % step, nbits(topo.mask(rel[0], core)))
+        landed(ap("fb%d" % step, S(NQ, NJ + NF)), "fa%d" % step, sum(nbits(topo.mask(c, core)) for c in rel[1:]))
+
+    a2 = ap("pi", S(0, 1))
+    op("g", lambda e: e.iota(a2[0], [[1, 1]], 0, 1), [], [a2])
+    a3 = ap("vv")
+    op("g", lambda e: e.iota(a3[0], [[1, 256]], 0, -1, allow_small_or_imprecise_dtypes=True), [], [a3])
+
+    fill(ap("plc0"), 2048.0)
+    fill(ap("mask0"), 0.0)
+    wa, wb, wz = 2 * rows_a[0], 32 - 2 * rows_a[0], 32 - 2 * rows_a[6]
+    fill(ap("sqr", S(0, wa), S(64, 80)), 0.0)
+    fill(ap("sqr", S(WMAX, WMAX + wz), S(64, 80)), 0.0)
+    ts(ap("pi", S(4, 5)), ap("pi", S(0, 1)), 15, None, ALU.bitwise_and)
+    for x in "AB":
+        fill(ap("m" + x, S(0, 1)), BIG)
+    r16 = ap("col", S(0, 1))
+    cp(r16, ap("pi", S(4, 5)))
+    for x in "AB":
+        fill(ap("c" + x, S(0, 1)), 0.0)
+    ne15, ne0, eq15, eq0, big15, big0 = [ap("col", S(i, i + 1)) for i in range(1, 7)]
+    ts(ne15, r16, 15.0, None, ALU.not_equal)
+    ts(eq15, r16, 15.0, None, ALU.is_equal)
+    ts(big0, r16, 0.0, BIG, ALU.is_equal, ALU.mult)
+    ts(ne0, r16, 0.0, None, ALU.not_equal)
+    ts(eq0, r16, 0.0, None, ALU.is_equal)
+    ts(big15, r16, 15.0, BIG, ALU.is_equal, ALU.mult)
+    v128 = ap("vv", S(0, 128))
+    spec = [(0.0, 1.0), (1.0, ne15), (-15.0, eq15), (-1.0, ne0), (15.0, eq0), (0.0, 32.0), (0.0, 64.0)]
+    mh = [ap("mh", S(128 * i, 128 * i + 128)) for i in range(5)]
+    mb = [ap("mb", S(128 * i, 128 * i + 128)) for i in range(7)]
+    mf = ap("mf")
+    for i in (0, 6, 5, 1, 2):
+        ts(mb[i], v128, spec[i][0], spec[i][1], ALU.is_equal, ALU.mult)
+    for i in (0, 1, 2):
+        ts(mh[i], v128, spec[i][0], spec[i][1], ALU.is_equal, ALU.mult)
+
+    aset(ap("plc0", allc, 5), 32, 2080.0)
+    for nm in ("floor", "d1", "mask1"):
+        aset(ap(nm), 160, 0.0)
+    aset(ap("plc1"), 256, 2048.0)
+    aset(ap("sqr", S(WMAX + wb, WMAX + wz), S(0, 16)), 16 * (wz - wb), 0.0)
+    aset(ap("mask0", S(4, 160, 5)), 32, BIG)
+    aset(ap("mask0", S(1, 160, 10)), 16, big0)
+    aset(ap("mask0", S(2, 10, 5)), 2, BIG)
+    aset(ap("floor", S(4, 160, 5)), 32, BIG)
+    aset(ap("d1", S(4, 160, 5)), 32, BIG)
+    aset(ap("plc1", allc, 5), 32, 2016.0)
+    aset(ap("mask1", S(0, 160, 5)), 32, -BIG)
+    aset(ap("mask1", S(4, 160, 5)), 32, BIG)
+    aset(ap("mask1", S(6, 160, 10)), 16, big15)
+    aset(ap("mask1", S(152, 160, 5)), 2, BIG)
+
+    ts(ap("jt", S(0, 64)), ap("jui"), 6, None, ALU.arith_shift_right)
+    ts(ap("jt", S(64, 128)), ap("jui"), 63, None, ALU.bitwise_and)
+    ts(ap("z0"), ap("sti"), -2048.0, None, ALU.add)
+    cp(ap("fb0", S(0, NJ)), ap("jt"))
+    ts(pst(0, 0, 32), ap("sti"), -2048.0, None, ALU.add)
+
+    sent = 0
+    for k, c in enumerate(relays_of(T, topo, core)):
+        a = ap("fb0", S(k * NQ, (k + 1) * NQ))
+        deps("g", [a], [])
+        rid, pid = topo.addr(c, core)
+        m = topo.mask(core, c)
+        g.remote_dma(a[0], a[0], T.sem.arr, T.sem.sent, pid, rid, m)
+        sent += nbits(m)
+
+    fs = [(rank + s) % n for s in range(n)]
+    for nm in ("mask7", "floor7", "dpf"):
+        gset(ap(nm), 256, 0)
+    gset(ap("mask7", allc, 7), 32, BIG)
+    gset(ap("mask7", S(30, 32), 5), 2, BIG)
+    gset(ap("floor7", S(7, 256, 8)), 32, BIG)
+    for sl, val in ((1, fs[0] - fs[1]), (2, fs[1] - fs[2]), (3, fs[2] - fs[3]), (7, fs[3])):
+        gset(ap("dpf", S(sl, 256, 8)), 32, val)
+
+    def flags(s, src, c0, c1):
+        o = 32 * s
+        base = 31.5 / 64
+        act(ap("a1", S(o + c0, o + c1)), src, ACT.Identity, bias=192.0 - base, scale=1.0 / 64)
+        if s % 2 == 0:
+            act(ap("na", S(o + c0, o + c1)), src, ACT.Identity, bias=-(191.0 - base + 1.0 / 64), scale=-1.0 / 64)
+            act(ap("sg", S(o + c0, o + c1)), src, ACT.Sign, bias=1983.5, scale=-1.0)
+        else:
+            act(ap("na", S(o + c0, o + c1)), src, ACT.Identity, bias=-(193.0 - base - 1.0 / 64), scale=-1.0 / 64)
+            act(ap("sg", S(o + c0, o + c1)), src, ACT.Sign, bias=-1984.5, scale=-1.0)
+
+    flags(0, ap("z0"), 0, 32)
+
+    tiles = []
+    for s in range(8):
+        tiles.append((s, "A", 0, 2 * rows_a[s]))
+        tiles.append((s, "B", 2 * rows_a[s], 32))
+
+    def lo_of(s):
+        return 0 if s == 7 else 3
+
+    def places_pre(tile):
+        s, x, c0, c1 = tile
+        w, t, lo, fb = c1 - c0, s % 2, lo_of(s), "fb%d" % (s // 2)
+        pl = "pl" + x
+        mm(ap(pl, S(0, w), S(lo, 8)), mb[0], ap("plc%d" % t, S(c0, c1), S(lo, 8)), start=True)
+        mm(ap(pl, S(0, w), 6), mb[6], ap(fb, S(32 * t + c0, 32 * t + c1)))
+        mm(ap(pl, S(0, w), 6), mb[0], ap(fb, S(64 + 32 * t + c0, 64 + 32 * t + c1)))
+        if s == 7:
+            for j in range(3):
+                mm(ap(pl, S(0, w), j), mh[0], pst(2 * j + 2, c0, c1))
+
+    def places(tile):
+        s, x, c0, c1 = tile
+        w, t, o = c1 - c0, s % 2, 32 * s
+        pl = "pl" + x
+        sh, wr = (1, 2) if t == 0 else (3, 4)
+        if t == 0:
+            wo, w0 = S(1, w, 2), c0
+            b0, b1, dc = max(c0, 2), c1, -2
+        else:
+            wo, w0 = S(0, w, 2), c0 + 1
+            b0, b1, dc = c0, min(c1, 30), 2
+        here, wi = S(o + c0, o + c1), S(o + w0, o + c1, 2)
+        vo, vi = S(b0 - c0, b1 - c0), S(o + b0 + dc, o + b1 + dc)
+        mm(ap(pl, S(0, w), 3), mh[0], pst(s, c0, c1))
+        mm(ap(pl, S(0, w), 6), mh[0], pst(s, c0, c1))
+        mm(ap(pl, vo, 5), mh[0], pst(s, b0 + dc, b1 + dc))
+        mm(ap(pl, S(0, w), 4), mh[sh], pst(s, c0, c1))
+        mm(ap(pl, wo, 4), mh[wr], pst(s, w0, c1, 2))
+        for nm in ("a1", "na"):
+            mm(ap(pl, S(0, w), 4), mb[sh], ap(nm, here))
+            mm(ap(pl, wo, 4), mb[wr], ap(nm, wi))
+        mm(ap(pl, vo, 5), mb[5], ap("sg", vi), stop=True)
+
+    def lists(tile):
+        s, x, c0, c1 = tile
+        w, nk, lo = c1 - c0, 4 - s % 2, lo_of(s)
+        m = (8 - lo) * w
+        ts(ap("lst" + x, S(0, nk * w)), ap("pl" + x, S(0, w), S(7 - nk, 7)), 0.0, 4095.0, ALU.max, ALU.min)
+        act(ap("t1" + x, S(0, m)), ap("pl" + x, S(0, w), S(lo, 8)), ACT.Relu)
+
+    def clamps(tile):
+        s, x, c0, c1 = tile
+        m = (8 - lo_of(s)) * (c1 - c0)
+        act(ap("c" + x, S(1, m + 1)), ap("t1" + x, S(0, m)), ACT.Relu, bias=4095.0, scale=-1.0)
+        act(ap("pc" + x, S(0, m)), ap("t1" + x, S(0, m)), ACT.Relu, bias=4095.0, scale=-1.0)
+
+    def squares(tile, u0, u1, src):
+        s, x, c0, c1 = tile
+        nk = 4 - s % 2
+        o = WMAX if x == "B" else 0
+        if s == 7:
+            act(ap("d" + x, S(16 * nk * u0, 16 * nk * u1)), src, ACT.Square)
+        else:
+            act(ap("sqr", S(o + u0, o + u1), S(64 - 16 * nk, 64)), src, ACT.Square)
+
+    def gather(tile, u0, u1):
+        s, x, c0, c1 = tile
+        nk = 4 - s % 2
+        win = ap("fb%d" % (s // 2), S(NJ, NJ + NF))
+        off = ap("lst" + x, S(nk * u0, nk * u1))
+        out = ap("d" + x, S(16 * nk * u0, 16 * nk * u1))
+        qq = ap("q%d" % nk, S(16 * nk * (c0 + u0), 16 * nk * (c0 + u1)))
+        op("v", lambda e: e.tensor_tensor(out[0], win[0].indirect(off[0]), qq[0], ALU.subtract), [win, off, qq], [out])
+        squares(tile, u0, u1, out)
+
+    def side_cols(tile):
+        return OPT["side"][tile[0] % 2]
+
+    def side_gather(tile):
+        s, x, c0, c1 = tile
+        nk, u = 4 - s % 2, side_cols(tile)
+        win = ap("fb%d" % (s // 2), S(NJ, NJ + NF))
+        off = ap("lst" + x, S(0, nk * u))
+        out = ap("gs", S(0, 16 * nk * u))
+        op("a", lambda e: e.activation(out[0], win[0].indirect(off[0]), ACT.Identity, bias=0.0, scale=-1.0),
+           [win, off], [out])
+
+    def side_diff(tile):
+        s, x, c0, c1 = tile
+        nk, u = 4 - s % 2, side_cols(tile)
+        m = 16 * nk * u
+        mm(ap("pg", S(0, m)), mb[0], ap("q%d" % nk, S(16 * nk * c0, 16 * nk * c0 + m)), start=True)
+        mm(ap("pg", S(0, m)), mb[0], ap("gs", S(0, m)), stop=True)
+
+    def diffs(tile):
+        s, x, c0, c1 = tile
+        m = (8 - lo_of(s)) * (c1 - c0)
+        tt(ap("dp" + x, S(0, m)), ap("pc" + x, S(0, m)), ap("c" + x, S(0, m)), ALU.subtract)
+
+    def sums_pre(tile):
+        s, x, c0, c1 = tile
+        w = c1 - c0
+        if s == 7:
+            mm(ap("p7", S(0, w), S(0, 8)), mb[0], ap("mask7", S(c0, c1), S(0, 8)), start=True)
+            mm(ap("p7", S(0, w), S(0, 4)), mf, ap("cf", S(4 * c0, 4 * c1)))
+        else:
+            mm(ap("ps" + x, S(0, 5 * w)), mb[0], ap("mask%d" % (s % 2), S(5 * c0, 5 * c1)), start=True)
+
+    def sums(tile):
+        s, x, c0, c1 = tile
+        w = c1 - c0
+        o = WMAX if x == "B" else 0
+        for r in range(16):
+            sel = ap("tsel", S(15 - r, 143 - r))
+            if s == 7:
+                mm(ap("p7", S(0, w), S(4, 7)), sel, ap("d" + x, S(r, 48 * w, 16)), stop=(r == 15))
+            else:
+                mm(ap("ps" + x, S(0, 5 * w)), sel, ap("sqr", S(o, o + w), S(r, 80, 16)), stop=(r == 15))
+
+    def least_costs(tile):
+        s, x, c0, c1 = tile
+        w, ns = c1 - c0, 8 - lo_of(s)
+        if s == 7:
+            cp(ap("ps" + x, S(0, 8 * w)), ap("p7", S(0, w), S(0, 8)))
+        fl = ap("floor7" if s == 7 else "d1" if s % 2 else "floor", S(ns * c0, ns * c1))
+        scan(ap("m" + x, S(1, ns * w + 1)), ap("ps" + x, S(0, ns * w)), fl, BIG, ALU.min, ALU.max)
+
+    def pick(tile):
+        s, x, c0, c1 = tile
+        w, ns = c1 - c0, 8 - lo_of(s)
+        m = ns * w
+        ni, dp = ap("ni" + x, S(0, m)), ap("dp" + x, S(0, m))
+        tt(ni, ap("ps" + x, S(0, m)), ap("m" + x, S(0, m)), ALU.is_ge)
+        least = ap("m" + x, S(ns - 1, m, ns))
+        if s == 7:
+            act(ap("oc", S(c0, c1)), least, ACT.Copy)
+        scan(ap("z" + x, S(0, m)), dp, ni, 0.0, ALU.add, ALU.mult)
+        zl = ap("z" + x, S(ns - 1, m, ns))
+        if s < 7:
+            o = 160 * (s + 1)
+            scan(ap("p16", S(o + 5 * c0, o + 5 * c1)), dp, ni, 0.0, ALU.add, ALU.mult)
+            flags(s + 1, zl, c0, c1)
+            if s in (0, 2, 4):
+                act(ap("d1", S(5 * c0, 5 * c1, 5)), least, ACT.Copy)
+            else:
+                j = 3 if s == 6 else (s - 1) // 2
+                act(ap("cf", S(4 * c0 + j, 4 * c1, 4)), least, ACT.Copy)
+        else:
+            scan(ap("zf" + x, S(0, m)), ap("dpf", S(8 * c0, 8 * c1)), ni, 0.0, ALU.add, ALU.mult)
+            act(ap("op", S(c0, c1)), zl, ACT.Identity, bias=2048.0)
+            cp(ap("of", S(c0, c1)), ap("zf" + x, S(ns - 1, m, ns)))
+
+    places_pre(tiles[0]); places(tiles[0])
+    places_pre(tiles[1]); places(tiles[1])
+    for k in range(4):
+        cp(ap("qrep", allc, S(16 * k, 16 * k + 16)), ap("q"))
+    lists(tiles[0]); lists(tiles[1])
+    clamps(tiles[0]); clamps(tiles[1])
+    ca, cb = tiles[0][3], tiles[2][3]
+    cp(ap("q4", S(0, 64 * ca)), ap("qrep", S(0, ca), S(0, 64)))
+    act(ap("q4", S(64 * ca, 2048)), ap("qrep", S(ca, 32), S(0, 64)), ACT.Copy)
+    cp(ap("q3", S(0, 48 * cb)), ap("qrep", S(0, cb), S(16, 64)))
+    act(ap("q3", S(48 * cb, 1536)), ap("qrep", S(cb, 32), S(16, 64)), ACT.Copy)
+    ts(ap("tsel"), ap("vv", S(0, 144)), r16, 15.0, ALU.add, ALU.is_equal)
+    for i in (3, 4):
+        ts(mh[i], v128, spec[i][0], spec[i][1], ALU.is_equal, ALU.mult)
+        ts(mb[i], v128, spec[i][0], spec[i][1], ALU.is_equal, ALU.mult)
+    ts(mf, v128, 0.0, None, ALU.is_equal)
+
+    nt = len(tiles)
+    for i in range(nt + 1):
+        if i < nt:
+            w, u = tiles[i][3] - tiles[i][2], side_cols(tiles[i])
+            al = 2 if tiles[i][0] % 2 else 1
+            mid = u + al * int(round(OPT["frac"] * (w - u) / al))
+            cuts = [u, mid, w] + [u + al * int(round(f * (w - u) / al)) for f in OPT["pre"]] + [w - v for v in OPT["tail"]]
+            cuts = sorted(set(cuts))
+            npre = cuts.index(mid)
+            if i == nt - 1:
+                cuts = [u] + [w - v for v in OPT["last"] if w - v > u] + [w]
+                npre = OPT["lastpre"]
+            if u and i == 0:
+                side_gather(tiles[i])
+            for j in range(npre):
+                gather(tiles[i], cuts[j], cuts[j + 1])
+        if i >= 1:
+            sums(tiles[i - 1])
+        if i < nt and u:
+            side_diff(tiles[i])
+        if i >= 1:
+            if i + 1 < nt:
+                places_pre(tiles[i + 1])
+            least_costs(tiles[i - 1])
+        if i < nt:
+            diffs(tiles[i])
+        if i >= 1:
+            pick(tiles[i - 1])
+            if i + 1 < nt:
+                places(tiles[i + 1])
+        if i == nt - 3:
+            aset(ap("mask7", S(1, 32, 2), 4), 16, big15)
+        if i < nt:
+            if u:
+                squares(tiles[i], 0, u, ap("pg", S(0, 16 * (4 - tiles[i][0] % 2) * u)))
+            sums_pre(tiles[i])
+            for j in range(npre, len(cuts) - 1):
+                gather(tiles[i], cuts[j], cuts[j + 1])
+        if 1 <= i and i + 1 < nt:
+            lists(tiles[i + 1])
+            clamps(tiles[i + 1])
+        if i + 1 < nt and side_cols(tiles[i + 1]):
+            side_gather(tiles[i + 1])
+
+    outs = []
+    a = ap("oc"); outs.append(dma("s", T.yc[:], a[0], "out0", [a], []))
+    a = ap("op"); outs.append(dma("a", T.yp[:], a[0], "out1", [a], []))
+    a = ap("of"); outs.append(dma("s", T.yf[:], a[0], "out2", [a], []))
+    finish("g", [("sent", sent, {})] + outs)
+
+
+def rank_program(g, core, T, topo):
+    rank = T.rank_of(core)
+    if rank is not None:
+        rank_body(g, core, T, topo, rank)
+        return
+    for src in T.cores:
+        rel = relays_of(T, topo, src)
+        if core in rel:
+            relay_program(g, core, T, topo, src, rel.index(core))

@@ -1,73 +1,81 @@
 import numpy as np
+from concourse.bass import DstId, RemoteDMATransfer
 from concourse.mybir import AluOpType, ActivationFunctionType
 
-NJ = 128
 NF = 4096
-NQ = (NJ + NF) // 4
+PAD = 64
+NB = NF + 2 * PAD
+NP = NB // 8
 BIG = 8192.0
-WMAX = 24
 OPT = {
     "rows0": 10,
-    "side": [3, 2],
-    "pre": [0.4],
-    "frac": 0.7,
-    "tail": [2],
-    "last": [12, 6, 2],
-    "lastpre": 1,
+    "side": [8, 0],
+    "after": [0, 0],
 }
+ROWS_A = [OPT["rows0"] - (s + 1) // 2 for s in range(8)]
+WMAX = max(max(2 * r, 32 - 2 * r) for r in ROWS_A)
+ND = 16 * WMAX + 32
+NM = 164
 
 SCRATCH = {
-    "fb0": ("sbuf", [128, NJ + NF], "bfloat16"),
-    "fb1": ("sbuf", [128, NJ + NF], "bfloat16"),
-    "fb2": ("sbuf", [128, NJ + NF], "bfloat16"),
-    "fb3": ("sbuf", [128, NJ + NF], "bfloat16"),
-    "q": ("sbuf", [128, 512], "bfloat16"),
-    "qrep": ("sbuf", [128, 32, 64], "bfloat16"),
-    "q4": ("sbuf", [128, 32 * 64], "bfloat16"),
-    "q3": ("sbuf", [128, 32 * 48], "bfloat16"),
-    "sqr": ("sbuf", [128, 2 * WMAX, 80], "bfloat16"),
-    "gs": ("sbuf", [128, 256], "bfloat16"),
+    "jb": ("sbuf", [128, 512], "bfloat16"),
+    "q": ("sbuf", [128, 544], "bfloat16"),
+    "gs": ("sbuf", [128, 16 * WMAX], "bfloat16"),
     "sti": ("sbuf", [128, 32], "int32"),
     "jui": ("sbuf", [128, 64], "int32"),
     "jt": ("sbuf", [128, 128], "int32"),
-    "vv": ("sbuf", [128, 256], "bfloat16"),
+    "xi": ("sbuf", [128, 32], "int32"),
+    "v0": ("sbuf", [128, 96], "float32"),
+    "vv": ("sbuf", [128, 320], "bfloat16"),
     "pi": ("sbuf", [128, 8], "int32"),
     "col": ("sbuf", [128, 8], "float32"),
     "tsel": ("sbuf", [128, 144], "bfloat16"),
-    "mh": ("sbuf", [128, 5 * 128], "float16"),
-    "mb": ("sbuf", [128, 7 * 128], "bfloat16"),
+    "base": ("sbuf", [128, 640], "bfloat16"),
+    "hp": ("sbuf", [128, 640], "float16"),
+    "hn": ("sbuf", [128, 640], "float16"),
+    "ep": ("sbuf", [128, 640], "float16"),
+    "en": ("sbuf", [128, 640], "float16"),
+    "bp": ("sbuf", [128, 640], "bfloat16"),
+    "bn": ("sbuf", [128, 640], "bfloat16"),
+    "i64": ("sbuf", [128, 256], "bfloat16"),
+    "h64": ("sbuf", [128, 128], "float16"),
     "mf": ("sbuf", [128, 128], "float32"),
     "mask0": ("sbuf", [128, 160], "bfloat16"),
     "mask1": ("sbuf", [128, 160], "bfloat16"),
     "mask7": ("sbuf", [128, 32, 8], "bfloat16"),
-    "plc0": ("sbuf", [128, 32, 8], "bfloat16"),
-    "plc1": ("sbuf", [128, 32, 8], "bfloat16"),
-    "floor": ("sbuf", [128, 160], "float32"),
-    "d1": ("sbuf", [128, 160], "float32"),
-    "floor7": ("sbuf", [128, 256], "float32"),
-    "dpf": ("sbuf", [128, 256], "float32"),
-    "cf": ("sbuf", [128, 128], "float32"),
-    "p16": ("sbuf", [128, 8 * 160], "float16"),
-    "z0": ("sbuf", [128, 32], "float32"),
-    "a1": ("sbuf", [128, 8 * 32], "bfloat16"),
-    "na": ("sbuf", [128, 8 * 32], "bfloat16"),
-    "sg": ("sbuf", [128, 8 * 32], "bfloat16"),
+    "ce0": ("sbuf", [128, 5 * WMAX], "bfloat16"),
+    "ce1": ("sbuf", [128, 5 * WMAX], "bfloat16"),
+    "ce7": ("sbuf", [128, 8 * WMAX], "bfloat16"),
+    "cq0": ("sbuf", [128, 3, 32], "bfloat16"),
+    "cq1": ("sbuf", [128, 3, 32], "bfloat16"),
+    "floor": ("sbuf", [128, 5 * WMAX], "float32"),
+    "floor7": ("sbuf", [128, 8 * WMAX], "float32"),
+    "dpf": ("sbuf", [128, 8 * WMAX], "float32"),
+    "u16": ("sbuf", [128, 24, 32], "uint16"),
+    "x16": ("sbuf", [128, 24, 32], "float16"),
+    "fl": ("sbuf", [128, 24, 32], "bfloat16"),
+    "mc": ("sbuf", [128, 7 * NM], "float32"),
+    "m7": ("sbuf", [128, 260], "float32"),
     "oc": ("sbuf", [128, 32], "float32"),
     "of": ("sbuf", [128, 32], "float32"),
     "op": ("sbuf", [128, 32], "float32"),
-    "p7": ("psum", [128, 64, 8], "float32"),
+    "pq": ("psum", [128, 16, 32], "float32"),
     "pg": ("psum", [128, 512], "float32"),
 }
+for _k in range(4):
+    SCRATCH["fb%d" % _k] = ("sbuf", [128, NB], "bfloat16")
 for _x in "AB":
-    SCRATCH["d" + _x] = ("sbuf", [128, WMAX * 64], "bfloat16")
-    SCRATCH["lst" + _x] = ("sbuf", [128, WMAX * 4], "uint16")
-    for _n in ("m", "c", "t1", "dp", "ni", "z", "zf"):
-        SCRATCH[_n + _x] = ("sbuf", [128, WMAX * 8 + 8], "float32")
+    SCRATCH["d" + _x] = ("sbuf", [128, 4, ND], "bfloat16")
+    SCRATCH["sq0" + _x] = ("sbuf", [128, WMAX, 80], "bfloat16")
+    SCRATCH["sq1" + _x] = ("sbuf", [128, WMAX, 80], "bfloat16")
+    SCRATCH["ni" + _x] = ("sbuf", [128, 8 * WMAX], "bfloat16")
+    SCRATCH["z" + _x] = ("sbuf", [128, 8 * WMAX], "float32")
+    SCRATCH["zf" + _x] = ("sbuf", [128, 8 * WMAX], "float32")
     SCRATCH["ps" + _x] = ("psum", [128, 512], "float32")
-    SCRATCH["pl" + _x] = ("psum", [128, 64, 8], "float32")
-    SCRATCH["pc" + _x] = ("psum", [128, 512], "float32")
+    SCRATCH["pe" + _x] = ("psum", [128, 512], "float32")
+    SCRATCH["p7" + _x] = ("psum", [128, 64, 8], "float32")
 
-SEMAPHORES = ["sv", "sa", "sp", "sq", "ld0", "ld1", "ld2", "ld3", "lj", "ls", "lq", "sent", "arr",
+SEMAPHORES = ["sv", "sa", "sp", "sq", "ld0", "ld1", "lp0", "lp1", "lj", "ls", "lq", "sent", "arrj", "arr0", "arr1",
               "fj1", "fj2", "fj3", "fa1", "fa2", "fa3", "out0", "out1", "out2"]
 
 
@@ -89,19 +97,45 @@ def nbits(m):
     return bin(m).count("1")
 
 
+def split_mask(topo, src, dst, parts):
+    e = topo.engines(src, dst)
+    k = len(e) // parts
+    return [sum(1 << x for x in e[i * k:(i + 1) * k]) for i in range(parts)]
+
+
+def transfer(topo, src, dst, mask, sem, a, b):
+    rid, pid = topo.addr(dst, src)
+    return RemoteDMATransfer(dst_ids=[DstId(rid=rid, pnc=pid)], dma_engine_mask=mask, remote_sem=sem, src=a, dst=b)
+
+
 def relay_program(g, core, T, topo, src, k):
     n = len(T.cores)
     r = T.rank_of(src)
-    part = T.fb0[:, k * NQ:(k + 1) * NQ]
-    g.wait_ge(T.sem.arr, nbits(topo.mask(src, core)))
+    cols = [slice((4 * h + k) * NP, (4 * h + k + 1) * NP) for h in range(2)]
+    got = nbits(split_mask(topo, src, core, 4)[k])
     total = 0
+    if k >= 1:
+        d = T.cores[(r - k) % n]
+        rid, pid = topo.addr(d, core)
+        m = topo.mask(core, d)
+        g.wait_ge(T.sem.arrj, got)
+        g.remote_dma(T.jb[:, 128 * k:128 * k + 128], T.jb[:, 0:128], T.sem["fj%d" % k], T.sem.sent, pid, rid, m)
+        total += nbits(m)
     for step in range(1, n):
         d = T.cores[(r - step) % n]
         rid, pid = topo.addr(d, core)
         m = topo.mask(core, d)
-        sem = T.sem[("fj%d" if k == 0 else "fa%d") % step]
-        g.remote_dma(T["fb%d" % step][:, k * NQ:(k + 1) * NQ], part, sem, T.sem.sent, pid, rid, m)
-        total += nbits(m)
+        sem = T.sem["fa%d" % step]
+        if step == 1:
+            for h in range(2):
+                g.wait_ge(T.sem["arr%d" % h], got)
+                g.remote_dma(T.fb1[:, cols[h]], T.fb0[:, cols[h]], sem, T.sem.sent, pid, rid, m)
+                total += nbits(m)
+        else:
+            ms = split_mask(topo, core, d, 2)
+            g.remote_dma_fused([transfer(topo, core, d, ms[h], sem, T.fb0[:, cols[h]], T["fb%d" % step][:, cols[h]])
+                                for h in range(2)], local_sem=T.sem.sent)
+            total += nbits(m)
     g.wait_ge(T.sem.sent, total)
 
 
@@ -197,7 +231,6 @@ def rank_body(g, core, T, topo, rank):
     ALU, ACT = AluOpType, ActivationFunctionType
     ap, op, dma, landed, deps, finish = make_emitter(g, T)
     S = slice
-    rows_a = [OPT["rows0"] - (s + 1) // 2 for s in range(8)]
 
     def ts(out, in0, s1, s2, o0, o1=None):
         a1 = s1[0] if isinstance(s1, tuple) else s1
@@ -233,40 +266,42 @@ def rank_body(g, core, T, topo, rank):
     def gset(out, cnt, val):
         op("g", lambda e: e.iota(out[0], [[0, cnt]], int(val), 0, allow_small_or_imprecise_dtypes=True), [], [out])
 
-    def pst(s, c0, c1, step=1):
-        return ap("p16", S(160 * s + 5 * c0 + 4, 160 * s + 5 * c1, 5 * step))
+    allc, allw = S(0, 32), S(0, WMAX)
+    rel = relays_of(T, topo, core)
 
-    allc = S(0, 32)
-
-    a = ap("jui"); dma("a", a[0], T.ju[:], "lj", [], [a])
+    a = ap("jui"); dma("s", a[0], T.ju[:], "lj", [], [a])
     a = ap("sti"); dma("a", a[0], T.st[:], "ls", [], [a])
-    a = ap("q"); dma("a", a[0], T.qu[:], "lq", [], [a])
-    for k in range(4):
-        lo, hi = max(k * NQ, NJ), (k + 1) * NQ
-        a = ap("fb0", S(lo, hi)); dma("s", a[0], T.fr[:, lo - NJ:hi - NJ], "ld%d" % k, [], [a])
+    a = ap("fb0", S(0, PAD)); dma("a", a[0], T.fr[:, 0:PAD], "lp0", [], [a])
+    a = ap("fb0", S(PAD + NF, NB)); dma("a", a[0], T.fr[:, NF - PAD:NF], "lp1", [], [a])
+    a = ap("q", S(16, 528)); dma("a", a[0], T.qu[:], "lq", [], [a])
+    for h in range(2):
+        lo, hi = h * NF // 2, (h + 1) * NF // 2
+        a = ap("fb0", S(PAD + lo, PAD + hi)); dma("s", a[0], T.fr[:, lo:hi], "ld%d" % h, [], [a])
     for step in range(1, n):
-        src = T.cores[(rank + step) % n]
-        rel = relays_of(T, topo, src)
-        landed(ap("fb%d" % step, S(0, NQ)), "fj%d" % step, nbits(topo.mask(rel[0], core)))
-        landed(ap("fb%d" % step, S(NQ, NJ + NF)), "fa%d" % step, sum(nbits(topo.mask(c, core)) for c in rel[1:]))
+        far = relays_of(T, topo, T.cores[(rank + step) % n])
+        landed(ap("jb", S(128 * step, 128 * step + 128)), "fj%d" % step, nbits(topo.mask(far[step], core)))
+        landed(ap("fb%d" % step), "fa%d" % step, (2 if step == 1 else 1) * sum(nbits(topo.mask(c, core)) for c in far))
 
     a2 = ap("pi", S(0, 1))
     op("g", lambda e: e.iota(a2[0], [[1, 1]], 0, 1), [], [a2])
     a3 = ap("vv")
-    op("g", lambda e: e.iota(a3[0], [[1, 256]], 0, -1, allow_small_or_imprecise_dtypes=True), [], [a3])
+    op("g", lambda e: e.iota(a3[0], [[1, 320]], 0, -1, allow_small_or_imprecise_dtypes=True), [], [a3])
+    gset(ap("sq1A", allw, S(0, 16)), 16 * WMAX, 0)
+    gset(ap("sq1A", allw, S(64, 80)), 16 * WMAX, 0)
 
-    fill(ap("plc0"), 2048.0)
-    fill(ap("mask0"), 0.0)
-    wa, wb, wz = 2 * rows_a[0], 32 - 2 * rows_a[0], 32 - 2 * rows_a[6]
-    fill(ap("sqr", S(0, wa), S(64, 80)), 0.0)
-    fill(ap("sqr", S(WMAX, WMAX + wz), S(64, 80)), 0.0)
+    K2 = (64.0 * 193, 64.0 * 191)
+    for t in range(2):
+        fill(ap("mask%d" % t), 0.0)
+        fill(ap("ce%d" % t), 0.0)
+        fill(ap("cq%d" % t), 0.0)
+    fill(ap("floor"), 0.0)
     ts(ap("pi", S(4, 5)), ap("pi", S(0, 1)), 15, None, ALU.bitwise_and)
-    for x in "AB":
-        fill(ap("m" + x, S(0, 1)), BIG)
+    fill(ap("mc", S(0, 7 * NM, NM)), BIG)
+    fill(ap("m7", S(0, 1)), BIG)
     r16 = ap("col", S(0, 1))
     cp(r16, ap("pi", S(4, 5)))
-    for x in "AB":
-        fill(ap("c" + x, S(0, 1)), 0.0)
+    fill(ap("q", S(0, 16)), 0.0)
+    fill(ap("q", S(528, 544)), 0.0)
     ne15, ne0, eq15, eq0, big15, big0 = [ap("col", S(i, i + 1)) for i in range(1, 7)]
     ts(ne15, r16, 15.0, None, ALU.not_equal)
     ts(eq15, r16, 15.0, None, ALU.is_equal)
@@ -275,285 +310,302 @@ def rank_body(g, core, T, topo, rank):
     ts(eq0, r16, 0.0, None, ALU.is_equal)
     ts(big15, r16, 15.0, BIG, ALU.is_equal, ALU.mult)
     v128 = ap("vv", S(0, 128))
-    spec = [(0.0, 1.0), (1.0, ne15), (-15.0, eq15), (-1.0, ne0), (15.0, eq0), (0.0, 32.0), (0.0, 64.0)]
-    mh = [ap("mh", S(128 * i, 128 * i + 128)) for i in range(5)]
-    mb = [ap("mb", S(128 * i, 128 * i + 128)) for i in range(7)]
-    mf = ap("mf")
-    for i in (0, 6, 5, 1, 2):
-        ts(mb[i], v128, spec[i][0], spec[i][1], ALU.is_equal, ALU.mult)
-    for i in (0, 1, 2):
-        ts(mh[i], v128, spec[i][0], spec[i][1], ALU.is_equal, ALU.mult)
-
-    aset(ap("plc0", allc, 5), 32, 2080.0)
-    for nm in ("floor", "d1", "mask1"):
-        aset(ap(nm), 160, 0.0)
-    aset(ap("plc1"), 256, 2048.0)
-    aset(ap("sqr", S(WMAX + wb, WMAX + wz), S(0, 16)), 16 * (wz - wb), 0.0)
-    aset(ap("mask0", S(4, 160, 5)), 32, BIG)
-    aset(ap("mask0", S(1, 160, 10)), 16, big0)
-    aset(ap("mask0", S(2, 10, 5)), 2, BIG)
-    aset(ap("floor", S(4, 160, 5)), 32, BIG)
-    aset(ap("d1", S(4, 160, 5)), 32, BIG)
-    aset(ap("plc1", allc, 5), 32, 2016.0)
-    aset(ap("mask1", S(0, 160, 5)), 32, -BIG)
-    aset(ap("mask1", S(4, 160, 5)), 32, BIG)
-    aset(ap("mask1", S(6, 160, 10)), 16, big15)
-    aset(ap("mask1", S(152, 160, 5)), 2, BIG)
+    for i, (k, c) in enumerate([(0.0, 1.0), (1.0, ne15), (-15.0, eq15), (-1.0, ne0), (15.0, eq0)]):
+        ts(ap("base", S(128 * i, 128 * i + 128)), v128, k, c, ALU.is_equal, ALU.mult)
 
     ts(ap("jt", S(0, 64)), ap("jui"), 6, None, ALU.arith_shift_right)
     ts(ap("jt", S(64, 128)), ap("jui"), 63, None, ALU.bitwise_and)
-    ts(ap("z0"), ap("sti"), -2048.0, None, ALU.add)
-    cp(ap("fb0", S(0, NJ)), ap("jt"))
-    ts(pst(0, 0, 32), ap("sti"), -2048.0, None, ALU.add)
+    ts(ap("xi"), ap("sti"), 63, None, ALU.bitwise_and)
+    cp(ap("jb", S(0, 128)), ap("jt"))
+
+    def mat(name, i):
+        return ap(name, S(128 * i, 128 * i + 128))
+
+    eye, mf, h64 = mat("base", 0), ap("mf"), ap("h64")
+    for x in "AB":
+        aset(ap("sq0" + x, allw, S(64, 80)), 16 * WMAX, 0.0)
+    aset(ap("sq0A", S(0, 2), S(32, 48)), 32, 0.0)
+    act(ap("bp"), ap("base"), ACT.Identity, scale=0.5)
+    act(ap("bn"), ap("base"), ACT.Identity, scale=-0.5)
+    act(mat("i64", 0), eye, ACT.Identity, scale=64.0)
+    act(mat("i64", 1), eye, ACT.Identity, scale=-64.0)
+    act(mf, eye, ACT.Identity)
+    aset(ap("mask0", S(1, 160, 10)), 16, big0)
+    aset(ap("mask1", S(6, 160, 10)), 16, big15)
+
+    SIDE = (253.0 / 256, -127.0 / 256)
+    ts(ap("v0", S(0, 32)), ap("xi"), -1.0 / 128, None, ALU.mult)
+    tt(ap("v0", S(64, 96)), ap("sti"), ap("jui", S(0, 32)), ALU.add)
+    cp(ap("u16", 0, allc), ap("sti"))
+    tt(ap("v0", S(32, 64)), ap("v0", S(0, 32)), ap("sti"), ALU.add)
+    ts(ap("u16", 2, allc), ap("v0", S(64, 96)), 0.0, 4095.0, ALU.max, ALU.min)
+    ts(ap("ep", S(0, 128)), eye, 1.0, None, ALU.mult)
+    ts(ap("u16", 1, allc), ap("v0", S(32, 64)), SIDE[0], None, ALU.add)
+    ts(h64, eye, 1.0 / 64, None, ALU.mult)
+    for t in range(2):
+        fill(ap("cq%d" % t, 2, allc), (32.5, 30.5)[t])
+        fill(ap("mask%d" % t, S(4, 160, 5)), BIG)
+        fill(ap("ce%d" % t, S(1, 5 * WMAX, 5)), -K2[t])
+        fill(ap("ce%d" % t, S(2, 5 * WMAX, 5)), K2[t])
+        fill(ap("ce%d" % t, S(3, 5 * WMAX, 5)), 1952.0)
+        fill(ap("ce%d" % t, S(4, 5 * WMAX, 5)), 0.25)
+    fill(ap("mask0", S(2, 10, 5)), BIG)
+    fill(ap("mask1", S(152, 160, 5)), BIG)
+    fill(ap("floor", S(4, 5 * WMAX, 5)), BIG)
+    ts(ap("hp"), ap("base"), 127.0 / 128, None, ALU.mult)
+    ts(ap("hn"), ap("base"), -127.0 / 128, None, ALU.mult)
+    ts(ap("tsel"), ap("vv", S(0, 144)), r16, 15.0, ALU.add, ALU.is_equal)
+    for x in "AB":
+        fill(ap("d" + x, 1, S(0, ND)), 0.0)
 
     sent = 0
-    for k, c in enumerate(relays_of(T, topo, core)):
-        a = ap("fb0", S(k * NQ, (k + 1) * NQ))
-        deps("g", [a], [])
-        rid, pid = topo.addr(c, core)
-        m = topo.mask(core, c)
-        g.remote_dma(a[0], a[0], T.sem.arr, T.sem.sent, pid, rid, m)
-        sent += nbits(m)
+    ms = split_mask(topo, core, rel[0], 4)
+    a = ap("jb", S(0, 128))
+    deps("g", [a], [])
+    g.remote_dma_fused([transfer(topo, core, rel[k], ms[k], T.sem.arrj, a[0], a[0]) for k in range(1, 4)],
+                       local_sem=T.sem.sent)
+    sent += sum(nbits(m) for m in ms[1:])
+    for h in range(2):
+        if h == 0:
+            gset(ap("sq1B", allw, S(0, 16)), 16 * WMAX, 0)
+        deps("g", [ap("fb0", S(4 * h * NP, 4 * (h + 1) * NP))], [])
+        trs = []
+        for k, c in enumerate(rel):
+            a = ap("fb0", S((4 * h + k) * NP, (4 * h + k + 1) * NP))
+            trs.append(transfer(topo, core, c, ms[k], T.sem["arr%d" % h], a[0], a[0]))
+        g.remote_dma_fused(trs, local_sem=T.sem.sent)
+        sent += sum(nbits(m) for m in ms)
+        if h == 0:
+            gset(ap("sq1B", allw, S(64, 80)), 16 * WMAX, 0)
+            gset(ap("sq1B", allw, S(32, 48)), 16 * WMAX, 0)
 
     fs = [(rank + s) % n for s in range(n)]
-    for nm in ("mask7", "floor7", "dpf"):
-        gset(ap(nm), 256, 0)
+    w8 = 8 * WMAX
+    gset(ap("mask7"), 256, 0)
+    for nm in ("floor7", "dpf", "ce7"):
+        gset(ap(nm), w8, 0)
     gset(ap("mask7", allc, 7), 32, BIG)
     gset(ap("mask7", S(30, 32), 5), 2, BIG)
-    gset(ap("floor7", S(7, 256, 8)), 32, BIG)
-    for sl, val in ((1, fs[0] - fs[1]), (2, fs[1] - fs[2]), (3, fs[2] - fs[3]), (7, fs[3])):
-        gset(ap("dpf", S(sl, 256, 8)), 32, val)
-
-    def flags(s, src, c0, c1):
-        o = 32 * s
-        base = 31.5 / 64
-        act(ap("a1", S(o + c0, o + c1)), src, ACT.Identity, bias=192.0 - base, scale=1.0 / 64)
-        if s % 2 == 0:
-            act(ap("na", S(o + c0, o + c1)), src, ACT.Identity, bias=-(191.0 - base + 1.0 / 64), scale=-1.0 / 64)
-            act(ap("sg", S(o + c0, o + c1)), src, ACT.Sign, bias=1983.5, scale=-1.0)
-        else:
-            act(ap("na", S(o + c0, o + c1)), src, ACT.Identity, bias=-(193.0 - base - 1.0 / 64), scale=-1.0 / 64)
-            act(ap("sg", S(o + c0, o + c1)), src, ACT.Sign, bias=-1984.5, scale=-1.0)
-
-    flags(0, ap("z0"), 0, 32)
+    gset(ap("floor7", S(7, w8, 8)), WMAX, BIG)
+    for sl, val in ((0, fs[0] - fs[1]), (1, fs[1] - fs[2]), (2, fs[2] - fs[3]), (6, fs[3])):
+        gset(ap("dpf", S(sl, w8, 8)), WMAX, val)
+    for sl, val in ((4, -K2[1]), (5, K2[1]), (6, 2048)):
+        gset(ap("ce7", S(sl, w8, 8)), WMAX, val)
 
     tiles = []
     for s in range(8):
-        tiles.append((s, "A", 0, 2 * rows_a[s]))
-        tiles.append((s, "B", 2 * rows_a[s], 32))
+        tiles.append((s, "A", 0, 2 * ROWS_A[s]))
+        tiles.append((s, "B", 2 * ROWS_A[s], 32))
 
-    def lo_of(s):
-        return 0 if s == 7 else 3
+    def exact(s, c0, c1):
+        ts(ap("x16", S(3 * s, 3 * s + 3), S(c0, c1)), ap("u16", S(3 * s, 3 * s + 3), S(c0, c1)), -2048.0, None, ALU.add)
 
-    def places_pre(tile):
+    def rows_in(s, c0, c1):
+        w = c1 - c0
+        mm(ap("pq", S(0, 3), S(0, w)), eye, ap("cq%d" % (s % 2), S(0, 3), S(0, w)), start=True)
+        mm(ap("pq", S(0, 2), S(0, w)), mat("ep", 0), ap("x16", S(3 * s, 3 * s + 3, 2), S(c0, c1)))
+        mm(ap("pq", 2, S(0, w)), h64, ap("x16", 3 * s, S(c0, c1)), stop=True)
+
+    def rows_out(s, c0, c1):
+        act(ap("fl", S(3 * s, 3 * s + 3), S(c0, c1)), ap("pq", S(0, 3), S(0, c1 - c0)), ACT.Identity,
+            bias=192.0 - 4031.0 / 8192, scale=1.0 / 64)
+
+    def steps(tile):
         s, x, c0, c1 = tile
-        w, t, lo, fb = c1 - c0, s % 2, lo_of(s), "fb%d" % (s // 2)
-        pl = "pl" + x
-        mm(ap(pl, S(0, w), S(lo, 8)), mb[0], ap("plc%d" % t, S(c0, c1), S(lo, 8)), start=True)
-        mm(ap(pl, S(0, w), 6), mb[6], ap(fb, S(32 * t + c0, 32 * t + c1)))
-        mm(ap(pl, S(0, w), 6), mb[0], ap(fb, S(64 + 32 * t + c0, 64 + 32 * t + c1)))
+        w, t = c1 - c0, s % 2
+        ns, o = (8, 3) if s == 7 else (5, 0)
+        pos, neg = ("ep", "en") if s == 7 else ("hp", "hn")
+        sh, wr, dc = (1, 2, -2) if t == 0 else (3, 4, 2)
+        b0, b1 = max(c0, -dc), min(c1, 32 - dc)
+        here, vert = (c0, c1, 1, 0), (b0, b1, 1, dc)
+        wrap = (c0 + 1, c1, 2, -1) if t == 0 else (c0, c1, 2, 1)
+        xt, ft = [], []
         if s == 7:
-            for j in range(3):
-                mm(ap(pl, S(0, w), j), mh[0], pst(2 * j + 2, c0, c1))
+            xt += [(j, 0, 3 * (2 * j + 2), here) for j in range(3)]
+        xt += [(o, 0, 3 * s, here), (o + 1, sh, 3 * s + 1, here), (o + 1, wr, 3 * s + 1, wrap),
+               (o + 2, 0, 3 * s, vert), (o + 3, 0, 3 * s + 2, here)]
+        if s < 7:
+            ft += [(0, 0, 3 * s, here), (1, sh, 3 * s, here), (1, wr, 3 * s, wrap), (2, 0, 3 * s, vert),
+                   (3, 0, 3 * s + 1, here)]
+        calls = []
 
-    def places(tile):
-        s, x, c0, c1 = tile
-        w, t, o = c1 - c0, s % 2, 32 * s
-        pl = "pl" + x
-        sh, wr = (1, 2) if t == 0 else (3, 4)
-        if t == 0:
-            wo, w0 = S(1, w, 2), c0
-            b0, b1, dc = max(c0, 2), c1, -2
-        else:
-            wo, w0 = S(0, w, 2), c0 + 1
-            b0, b1, dc = c0, min(c1, 30), 2
-        here, wi = S(o + c0, o + c1), S(o + w0, o + c1, 2)
-        vo, vi = S(b0 - c0, b1 - c0), S(o + b0 + dc, o + b1 + dc)
-        mm(ap(pl, S(0, w), 3), mh[0], pst(s, c0, c1))
-        mm(ap(pl, S(0, w), 6), mh[0], pst(s, c0, c1))
-        mm(ap(pl, vo, 5), mh[0], pst(s, b0 + dc, b1 + dc))
-        mm(ap(pl, S(0, w), 4), mh[sh], pst(s, c0, c1))
-        mm(ap(pl, wo, 4), mh[wr], pst(s, w0, c1, 2))
-        for nm in ("a1", "na"):
-            mm(ap(pl, S(0, w), 4), mb[sh], ap(nm, here))
-            mm(ap(pl, wo, 4), mb[wr], ap(nm, wi))
-        mm(ap(pl, vo, 5), mb[5], ap("sg", vi), stop=True)
+        def add(k, plus, minus, src, row, span):
+            a0, a1, st, d = span
+            rhs = ap(src, row, S(a0 + d, a1 + d if st == 1 else a1, st))
+            cnt = len(range(a0, a1, st))
+            for slot, lhs in ((k, plus), (k - 1, minus)):
+                if slot >= 0:
+                    first = ns * (a0 - c0) + slot
+                    calls.append((ap("pe" + x, S(first, first + ns * st * (cnt - 1) + 1, ns * st)), lhs, rhs))
 
-    def lists(tile):
-        s, x, c0, c1 = tile
-        w, nk, lo = c1 - c0, 4 - s % 2, lo_of(s)
-        m = (8 - lo) * w
-        ts(ap("lst" + x, S(0, nk * w)), ap("pl" + x, S(0, w), S(7 - nk, 7)), 0.0, 4095.0, ALU.max, ALU.min)
-        act(ap("t1" + x, S(0, m)), ap("pl" + x, S(0, w), S(lo, 8)), ACT.Relu)
+        for k, m, row, span in xt:
+            add(k, mat(pos, m), mat(neg, m), "x16", row, span)
+        for k, m, row, span in ft:
+            add(k, mat("bp", m), mat("bn", m), "fl", row, span)
+        add(o + 2, mat("i64", 1), mat("i64", 0), "fl", 3 * s + 2, vert)
+        mm(ap("pe" + x, S(0, ns * w)), eye, ap("ce7" if s == 7 else "ce%d" % t, S(0, ns * w)), start=True)
+        for i, c in enumerate(calls):
+            mm(c[0], c[1], c[2], stop=(s == 7 and i == len(calls) - 1))
 
-    def clamps(tile):
+    def jumps(tile):
         s, x, c0, c1 = tile
-        m = (8 - lo_of(s)) * (c1 - c0)
-        act(ap("c" + x, S(1, m + 1)), ap("t1" + x, S(0, m)), ACT.Relu, bias=4095.0, scale=-1.0)
-        act(ap("pc" + x, S(0, m)), ap("t1" + x, S(0, m)), ACT.Relu, bias=4095.0, scale=-1.0)
+        if s < 7:
+            j = 128 * ((s + 1) // 2) + 32 * (1 - s % 2)
+            out = ap("pe" + x, S(4, 5 * (c1 - c0), 5))
+            mm(out, mat("i64", 0), ap("jb", S(j + c0, j + c1)))
+            mm(out, eye, ap("jb", S(j + 64 + c0, j + 64 + c1)), stop=True)
 
-    def squares(tile, u0, u1, src):
+    def gather(tile, k, u0=0):
         s, x, c0, c1 = tile
-        nk = 4 - s % 2
-        o = WMAX if x == "B" else 0
-        if s == 7:
-            act(ap("d" + x, S(16 * nk * u0, 16 * nk * u1)), src, ACT.Square)
-        else:
-            act(ap("sqr", S(o + u0, o + u1), S(64 - 16 * nk, 64)), src, ACT.Square)
-
-    def gather(tile, u0, u1):
-        s, x, c0, c1 = tile
-        nk = 4 - s % 2
-        win = ap("fb%d" % (s // 2), S(NJ, NJ + NF))
-        off = ap("lst" + x, S(nk * u0, nk * u1))
-        out = ap("d" + x, S(16 * nk * u0, 16 * nk * u1))
-        qq = ap("q%d" % nk, S(16 * nk * (c0 + u0), 16 * nk * (c0 + u1)))
+        t, fb = s % 2, "fb%d" % (s // 2)
+        a0, a1, row, base, sh, dc = c0 + u0, c1, 0, PAD, 0, 0
+        if k == 1:
+            row, sh = 1, 1 - 2 * t
+        if k == 2:
+            dc = -2 if t == 0 else 2
+            a0, a1, base = max(c0, -dc), min(c1, 32 - dc), PAD * (2 - 2 * t)
+        if k == 3:
+            row = 2
+        m, o = 16 * (a1 - a0), 16 + 16 * (a0 - c0)
+        win = ap(fb, S(base, base + NF))
+        off = ap("u16", 3 * s + row, S(a0 + dc, a1 + dc))
+        out = ap("d" + x, k, S(o + sh, o + sh + m))
+        qq = ap("q", S(16 + 16 * a0 + sh, 16 + 16 * a0 + sh + m))
         op("v", lambda e: e.tensor_tensor(out[0], win[0].indirect(off[0]), qq[0], ALU.subtract), [win, off, qq], [out])
-        squares(tile, u0, u1, out)
+        act(ap("sq%d%s" % (t, x), S(a0 - c0, a1 - c0), S(16 * k, 16 * k + 16)), ap("d" + x, k, S(o, o + m)), ACT.Square)
 
     def side_cols(tile):
-        return OPT["side"][tile[0] % 2]
+        return min(OPT["side"][tile[0] % 2], tile[3] - tile[2])
 
     def side_gather(tile):
         s, x, c0, c1 = tile
-        nk, u = 4 - s % 2, side_cols(tile)
-        win = ap("fb%d" % (s // 2), S(NJ, NJ + NF))
-        off = ap("lst" + x, S(0, nk * u))
-        out = ap("gs", S(0, 16 * nk * u))
+        u = side_cols(tile)
+        win = ap("fb%d" % (s // 2), S(PAD, PAD + NF))
+        off = ap("u16", 3 * s + 2, S(c0, c0 + u))
+        out = ap("gs", S(0, 16 * u))
         op("a", lambda e: e.activation(out[0], win[0].indirect(off[0]), ACT.Identity, bias=0.0, scale=-1.0),
            [win, off], [out])
 
     def side_diff(tile):
         s, x, c0, c1 = tile
-        nk, u = 4 - s % 2, side_cols(tile)
-        m = 16 * nk * u
-        mm(ap("pg", S(0, m)), mb[0], ap("q%d" % nk, S(16 * nk * c0, 16 * nk * c0 + m)), start=True)
-        mm(ap("pg", S(0, m)), mb[0], ap("gs", S(0, m)), stop=True)
+        m = 16 * side_cols(tile)
+        mm(ap("pg", S(0, m)), eye, ap("q", S(16 + 16 * c0, 16 + 16 * c0 + m)), start=True)
+        mm(ap("pg", S(0, m)), eye, ap("gs", S(0, m)), stop=True)
 
-    def diffs(tile):
+    def side_square(tile):
         s, x, c0, c1 = tile
-        m = (8 - lo_of(s)) * (c1 - c0)
-        tt(ap("dp" + x, S(0, m)), ap("pc" + x, S(0, m)), ap("c" + x, S(0, m)), ALU.subtract)
+        u = side_cols(tile)
+        act(ap("sq%d%s" % (s % 2, x), S(0, u), S(48, 64)), ap("pg", S(0, 16 * u)), ACT.Square)
+
+    def least(s, c0, c1):
+        return ap("mc", S(NM * s + 5 * c0 + 4, NM * s + 5 * c1, 5))
 
     def sums_pre(tile):
         s, x, c0, c1 = tile
         w = c1 - c0
         if s == 7:
-            mm(ap("p7", S(0, w), S(0, 8)), mb[0], ap("mask7", S(c0, c1), S(0, 8)), start=True)
-            mm(ap("p7", S(0, w), S(0, 4)), mf, ap("cf", S(4 * c0, 4 * c1)))
+            mm(ap("p7" + x, S(0, w), S(0, 8)), eye, ap("mask7", S(c0, c1), S(0, 8)), start=True)
+            for j, sj in enumerate((1, 3, 5, 6)):
+                mm(ap("p7" + x, S(0, w), j), mf, least(sj, c0, c1))
         else:
-            mm(ap("ps" + x, S(0, 5 * w)), mb[0], ap("mask%d" % (s % 2), S(5 * c0, 5 * c1)), start=True)
+            mm(ap("ps" + x, S(0, 5 * w)), eye, ap("mask%d" % (s % 2), S(5 * c0, 5 * c1)), start=True)
+            if s % 2:
+                mm(ap("ps" + x, S(0, 5 * w, 5)), mf, least(s - 1, c0, c1))
 
     def sums(tile):
         s, x, c0, c1 = tile
         w = c1 - c0
-        o = WMAX if x == "B" else 0
         for r in range(16):
             sel = ap("tsel", S(15 - r, 143 - r))
             if s == 7:
-                mm(ap("p7", S(0, w), S(4, 7)), sel, ap("d" + x, S(r, 48 * w, 16)), stop=(r == 15))
+                mm(ap("p7" + x, S(0, w), S(4, 7)), sel, ap("sq1" + x, S(0, w), S(16 + r, 64, 16)), stop=(r == 15))
             else:
-                mm(ap("ps" + x, S(0, 5 * w)), sel, ap("sqr", S(o, o + w), S(r, 80, 16)), stop=(r == 15))
-
-    def least_costs(tile):
-        s, x, c0, c1 = tile
-        w, ns = c1 - c0, 8 - lo_of(s)
-        if s == 7:
-            cp(ap("ps" + x, S(0, 8 * w)), ap("p7", S(0, w), S(0, 8)))
-        fl = ap("floor7" if s == 7 else "d1" if s % 2 else "floor", S(ns * c0, ns * c1))
-        scan(ap("m" + x, S(1, ns * w + 1)), ap("ps" + x, S(0, ns * w)), fl, BIG, ALU.min, ALU.max)
+                mm(ap("ps" + x, S(0, 5 * w)), sel, ap("sq%d%s" % (s % 2, x), S(0, w), S(r, 80, 16)), stop=(r == 15))
 
     def pick(tile):
         s, x, c0, c1 = tile
-        w, ns = c1 - c0, 8 - lo_of(s)
+        w, ns = c1 - c0, 8 if s == 7 else 5
         m = ns * w
-        ni, dp = ap("ni" + x, S(0, m)), ap("dp" + x, S(0, m))
-        tt(ni, ap("ps" + x, S(0, m)), ap("m" + x, S(0, m)), ALU.is_ge)
-        least = ap("m" + x, S(ns - 1, m, ns))
-        if s == 7:
-            act(ap("oc", S(c0, c1)), least, ACT.Copy)
-        scan(ap("z" + x, S(0, m)), dp, ni, 0.0, ALU.add, ALU.mult)
-        zl = ap("z" + x, S(ns - 1, m, ns))
-        if s < 7:
-            o = 160 * (s + 1)
-            scan(ap("p16", S(o + 5 * c0, o + 5 * c1)), dp, ni, 0.0, ALU.add, ALU.mult)
-            flags(s + 1, zl, c0, c1)
-            if s in (0, 2, 4):
-                act(ap("d1", S(5 * c0, 5 * c1, 5)), least, ACT.Copy)
-            else:
-                j = 3 if s == 6 else (s - 1) // 2
-                act(ap("cf", S(4 * c0 + j, 4 * c1, 4)), least, ACT.Copy)
-        else:
-            scan(ap("zf" + x, S(0, m)), ap("dpf", S(8 * c0, 8 * c1)), ni, 0.0, ALU.add, ALU.mult)
-            act(ap("op", S(c0, c1)), zl, ACT.Identity, bias=2048.0)
-            cp(ap("of", S(c0, c1)), ap("zf" + x, S(ns - 1, m, ns)))
+        mb, mo = ("m7", ns * c0) if s == 7 else ("mc", NM * s + ns * c0)
+        ps, ni, z = ap("ps" + x, S(0, m)), ap("ni" + x, S(0, m)), ap("z" + x, S(0, m))
 
-    places_pre(tiles[0]); places(tiles[0])
-    places_pre(tiles[1]); places(tiles[1])
-    for k in range(4):
-        cp(ap("qrep", allc, S(16 * k, 16 * k + 16)), ap("q"))
-    lists(tiles[0]); lists(tiles[1])
-    clamps(tiles[0]); clamps(tiles[1])
-    ca, cb = tiles[0][3], tiles[2][3]
-    cp(ap("q4", S(0, 64 * ca)), ap("qrep", S(0, ca), S(0, 64)))
-    act(ap("q4", S(64 * ca, 2048)), ap("qrep", S(ca, 32), S(0, 64)), ACT.Copy)
-    cp(ap("q3", S(0, 48 * cb)), ap("qrep", S(0, cb), S(16, 64)))
-    act(ap("q3", S(48 * cb, 1536)), ap("qrep", S(cb, 32), S(16, 64)), ACT.Copy)
-    ts(ap("tsel"), ap("vv", S(0, 144)), r16, 15.0, ALU.add, ALU.is_equal)
-    for i in (3, 4):
-        ts(mh[i], v128, spec[i][0], spec[i][1], ALU.is_equal, ALU.mult)
-        ts(mb[i], v128, spec[i][0], spec[i][1], ALU.is_equal, ALU.mult)
-    ts(mf, v128, 0.0, None, ALU.is_equal)
+        def one():
+            if s == 7:
+                cp(ps, ap("p7" + x, S(0, w), S(0, 8)))
+            scan(ap(mb, S(mo + 1, mo + 1 + m)), ps, ap("floor7" if s == 7 else "floor", S(0, m)), BIG, ALU.min, ALU.max)
 
+        def two():
+            tt(ni, ps, ap(mb, S(mo, mo + m)), ALU.is_ge)
+            if s == 7:
+                act(ap("oc", S(c0, c1)), ap(mb, S(mo + 7, mo + m, 8)), ACT.Copy)
+
+        def three():
+            scan(z, ni, ap("pe" + x, S(0, m)), 0.0, ALU.mult, ALU.add)
+            if s == 7:
+                scan(ap("zf" + x, S(0, m)), ni, ap("dpf", S(0, m)), 0.0, ALU.mult, ALU.add)
+
+        def four():
+            if s == 7:
+                act(ap("op", S(c0, c1)), ap("z" + x, S(6, m, 8)), ACT.Copy)
+                cp(ap("of", S(c0, c1)), ap("zf" + x, S(6, m, 8)))
+                return
+            v, r = ap("z" + x, S(3, m, 5)), 3 * (s + 1)
+            ts(ap("u16", r + 2, S(c0, c1)), ap("z" + x, S(4, m, 5)), 0.0, 4095.0, ALU.max, ALU.min)
+            ts(ap("u16", r, S(c0, c1)), v, 0.25, None, ALU.add)
+            ts(ap("u16", r + 1, S(c0, c1)), v, SIDE[(s + 1) % 2], None, ALU.add)
+
+        return [one, two, three, four]
+
+    exact(0, 0, 32)
+    rows_in(0, 0, 32)
+    rows_out(0, 0, 32)
     nt = len(tiles)
     for i in range(nt + 1):
-        if i < nt:
-            w, u = tiles[i][3] - tiles[i][2], side_cols(tiles[i])
-            al = 2 if tiles[i][0] % 2 else 1
-            mid = u + al * int(round(OPT["frac"] * (w - u) / al))
-            cuts = [u, mid, w] + [u + al * int(round(f * (w - u) / al)) for f in OPT["pre"]] + [w - v for v in OPT["tail"]]
-            cuts = sorted(set(cuts))
-            npre = cuts.index(mid)
-            if i == nt - 1:
-                cuts = [u] + [w - v for v in OPT["last"] if w - v > u] + [w]
-                npre = OPT["lastpre"]
-            if u and i == 0:
-                side_gather(tiles[i])
-            for j in range(npre):
-                gather(tiles[i], cuts[j], cuts[j + 1])
-        if i >= 1:
-            sums(tiles[i - 1])
-        if i < nt and u:
-            side_diff(tiles[i])
-        if i >= 1:
-            if i + 1 < nt:
-                places_pre(tiles[i + 1])
-            least_costs(tiles[i - 1])
-        if i < nt:
-            diffs(tiles[i])
-        if i >= 1:
-            pick(tiles[i - 1])
-            if i + 1 < nt:
-                places(tiles[i + 1])
-        if i == nt - 3:
-            aset(ap("mask7", S(1, 32, 2), 4), 16, big15)
-        if i < nt:
+        tile = tiles[i] if i < nt else None
+        prev = tiles[i - 1] if i >= 1 else None
+        made = tiles[i - 2] if 2 <= i < nt else None
+        todo = pick(prev) if prev else []
+        if tile:
+            t, u = tile[0] % 2, side_cols(tile)
+            order = [(2, 0)] + ([(0, 0)] if t == 0 else []) + [(1, 0)] + ([(3, u)] if u < tile[3] - tile[2] else [])
+            late = OPT["after"][t] if prev else 0
             if u:
-                squares(tiles[i], 0, u, ap("pg", S(0, 16 * (4 - tiles[i][0] % 2) * u)))
-            sums_pre(tiles[i])
-            for j in range(npre, len(cuts) - 1):
-                gather(tiles[i], cuts[j], cuts[j + 1])
-        if 1 <= i and i + 1 < nt:
-            lists(tiles[i + 1])
-            clamps(tiles[i + 1])
-        if i + 1 < nt and side_cols(tiles[i + 1]):
-            side_gather(tiles[i + 1])
+                side_gather(tile)
+            if prev:
+                sums(prev)
+                jumps(prev)
+            if u:
+                side_diff(tile)
+            for j, (k, u0) in enumerate(order):
+                if j >= len(order) - late:
+                    todo.pop(0)()
+                gather(tile, k, u0)
+                if j == 0:
+                    if made:
+                        exact(tile[0], made[2], made[3])
+                        rows_in(tile[0], made[2], made[3])
+                    if u:
+                        side_square(tile)
+                    if i == nt - 3:
+                        ts(ap("ep", S(128, 640)), ap("base", S(128, 640)), 1.0, None, ALU.mult)
+                        ts(ap("en"), ap("base"), -1.0, None, ALU.mult)
+                        aset(ap("mask7", S(1, 32, 2), 4), 16, big15)
+                    sums_pre(tile)
+                if j == 1:
+                    if made:
+                        rows_out(tile[0], made[2], made[3])
+                    steps(tile)
+        else:
+            sums(prev)
+        for f in todo:
+            f()
 
     outs = []
     a = ap("oc"); outs.append(dma("s", T.yc[:], a[0], "out0", [a], []))
     a = ap("op"); outs.append(dma("a", T.yp[:], a[0], "out1", [a], []))
     a = ap("of"); outs.append(dma("s", T.yf[:], a[0], "out2", [a], []))
-    finish("g", [("sent", sent, {})] + outs)
+    waits = [("fj%d" % k, nbits(topo.mask(relays_of(T, topo, T.cores[(rank + k) % n])[k], core)), {}) for k in range(1, n)]
+    finish("g", [("sent", sent, {})] + waits + outs)
 
 
 def rank_program(g, core, T, topo):

@@ -5,12 +5,17 @@ from concourse.mybir import AluOpType, ActivationFunctionType
 NF = 4096
 PAD = 64
 NB = NF + 2 * PAD
-NP = NB // 8
+LEAD = 2 * PAD
+NP = (NB - LEAD) // 8
 BIG = 8192.0
+OFF = 2048.0
 OPT = {
     "rows0": 10,
-    "side": [8, 0],
-    "after": [0, 0],
+    "side": [20, 14],
+    "last": "asgxrdfomegqG",
+    "plan": ["asgdfgqpxrgpmeGpop", "asgdfgqpxrgpmeGpop"],
+    "cut": [0, 0],
+    "split": 0,
 }
 ROWS_A = [OPT["rows0"] - (s + 1) // 2 for s in range(8)]
 WMAX = max(max(2 * r, 32 - 2 * r) for r in ROWS_A)
@@ -31,15 +36,8 @@ SCRATCH = {
     "col": ("sbuf", [128, 8], "float32"),
     "tsel": ("sbuf", [128, 144], "bfloat16"),
     "base": ("sbuf", [128, 640], "bfloat16"),
-    "hp": ("sbuf", [128, 640], "float16"),
-    "hn": ("sbuf", [128, 640], "float16"),
-    "ep": ("sbuf", [128, 640], "float16"),
-    "en": ("sbuf", [128, 640], "float16"),
-    "bp": ("sbuf", [128, 640], "bfloat16"),
-    "bn": ("sbuf", [128, 640], "bfloat16"),
-    "i64": ("sbuf", [128, 256], "bfloat16"),
-    "h64": ("sbuf", [128, 128], "float16"),
-    "mf": ("sbuf", [128, 128], "float32"),
+    "nbase": ("sbuf", [128, 640], "bfloat16"),
+    "diag": ("sbuf", [128, 896], "bfloat16"),
     "mask0": ("sbuf", [128, 160], "bfloat16"),
     "mask1": ("sbuf", [128, 160], "bfloat16"),
     "mask7": ("sbuf", [128, 32, 8], "bfloat16"),
@@ -54,7 +52,7 @@ SCRATCH = {
     "u16": ("sbuf", [128, 24, 32], "uint16"),
     "x16": ("sbuf", [128, 24, 32], "float16"),
     "fl": ("sbuf", [128, 24, 32], "bfloat16"),
-    "mc": ("sbuf", [128, 7 * NM], "float32"),
+    "mc": ("sbuf", [128, 7 * NM], "float16"),
     "m7": ("sbuf", [128, 260], "float32"),
     "oc": ("sbuf", [128, 32], "float32"),
     "of": ("sbuf", [128, 32], "float32"),
@@ -75,7 +73,7 @@ for _x in "AB":
     SCRATCH["pe" + _x] = ("psum", [128, 512], "float32")
     SCRATCH["p7" + _x] = ("psum", [128, 64, 8], "float32")
 
-SEMAPHORES = ["sv", "sa", "sp", "sq", "ld0", "ld1", "lp0", "lp1", "lj", "ls", "lq", "sent", "arrj", "arr0", "arr1",
+SEMAPHORES = ["sv", "sa", "sp", "sq", "ld0", "ld1", "lp", "lj", "ls", "lq", "sent", "arrj", "arr0", "arr1",
               "fj1", "fj2", "fj3", "fa1", "fa2", "fa3", "out0", "out1", "out2"]
 
 
@@ -111,14 +109,14 @@ def transfer(topo, src, dst, mask, sem, a, b):
 def relay_program(g, core, T, topo, src, k):
     n = len(T.cores)
     r = T.rank_of(src)
-    cols = [slice((4 * h + k) * NP, (4 * h + k + 1) * NP) for h in range(2)]
+    cols = [slice(LEAD + (4 * h + k) * NP, LEAD + (4 * h + k + 1) * NP) for h in range(2)]
     got = nbits(split_mask(topo, src, core, 4)[k])
     total = 0
+    g.wait_ge(T.sem.arrj, got)
     if k >= 1:
         d = T.cores[(r - k) % n]
         rid, pid = topo.addr(d, core)
         m = topo.mask(core, d)
-        g.wait_ge(T.sem.arrj, got)
         g.remote_dma(T.jb[:, 128 * k:128 * k + 128], T.jb[:, 0:128], T.sem["fj%d" % k], T.sem.sent, pid, rid, m)
         total += nbits(m)
     for step in range(1, n):
@@ -126,6 +124,9 @@ def relay_program(g, core, T, topo, src, k):
         rid, pid = topo.addr(d, core)
         m = topo.mask(core, d)
         sem = T.sem["fa%d" % step]
+        if k == 0:
+            g.remote_dma(T["fb%d" % step][:, 0:LEAD], T.fb0[:, 0:LEAD], sem, T.sem.sent, pid, rid, m)
+            total += nbits(m)
         if step == 1:
             for h in range(2):
                 g.wait_ge(T.sem["arr%d" % h], got)
@@ -271,16 +272,15 @@ def rank_body(g, core, T, topo, rank):
 
     a = ap("jui"); dma("s", a[0], T.ju[:], "lj", [], [a])
     a = ap("sti"); dma("a", a[0], T.st[:], "ls", [], [a])
-    a = ap("fb0", S(0, PAD)); dma("a", a[0], T.fr[:, 0:PAD], "lp0", [], [a])
-    a = ap("fb0", S(PAD + NF, NB)); dma("a", a[0], T.fr[:, NF - PAD:NF], "lp1", [], [a])
+    a = ap("fb0", S(PAD, LEAD)); dma("a", a[0], T.fr[:, 0:PAD], "lp", [], [a])
     a = ap("q", S(16, 528)); dma("a", a[0], T.qu[:], "lq", [], [a])
     for h in range(2):
-        lo, hi = h * NF // 2, (h + 1) * NF // 2
-        a = ap("fb0", S(PAD + lo, PAD + hi)); dma("s", a[0], T.fr[:, lo:hi], "ld%d" % h, [], [a])
+        lo, hi = LEAD + 4 * h * NP, min(LEAD + 4 * (h + 1) * NP, PAD + NF)
+        a = ap("fb0", S(lo, hi)); dma("s", a[0], T.fr[:, lo - PAD:hi - PAD], "ld%d" % h, [], [a])
     for step in range(1, n):
         far = relays_of(T, topo, T.cores[(rank + step) % n])
         landed(ap("jb", S(128 * step, 128 * step + 128)), "fj%d" % step, nbits(topo.mask(far[step], core)))
-        landed(ap("fb%d" % step), "fa%d" % step, (2 if step == 1 else 1) * sum(nbits(topo.mask(c, core)) for c in far))
+        landed(ap("fb%d" % step), "fa%d" % step, (9 if step == 1 else 5) * nbits(topo.mask(far[0], core)))
 
     a2 = ap("pi", S(0, 1))
     op("g", lambda e: e.iota(a2[0], [[1, 1]], 0, 1), [], [a2])
@@ -289,12 +289,12 @@ def rank_body(g, core, T, topo, rank):
     gset(ap("sq1A", allw, S(0, 16)), 16 * WMAX, 0)
     gset(ap("sq1A", allw, S(64, 80)), 16 * WMAX, 0)
 
-    K2 = (64.0 * 193, 64.0 * 191)
+    K2 = (193.0, 191.0)
     for t in range(2):
-        fill(ap("mask%d" % t), 0.0)
+        fill(ap("mask%d" % t), -OFF)
         fill(ap("ce%d" % t), 0.0)
         fill(ap("cq%d" % t), 0.0)
-    fill(ap("floor"), 0.0)
+    fill(ap("floor"), -BIG)
     ts(ap("pi", S(4, 5)), ap("pi", S(0, 1)), 15, None, ALU.bitwise_and)
     fill(ap("mc", S(0, 7 * NM, NM)), BIG)
     fill(ap("m7", S(0, 1)), BIG)
@@ -309,6 +309,7 @@ def rank_body(g, core, T, topo, rank):
     ts(ne0, r16, 0.0, None, ALU.not_equal)
     ts(eq0, r16, 0.0, None, ALU.is_equal)
     ts(big15, r16, 15.0, BIG, ALU.is_equal, ALU.mult)
+    ts(ap("col", S(5, 7)), ap("col", S(5, 7)), -OFF, None, ALU.add)
     v128 = ap("vv", S(0, 128))
     for i, (k, c) in enumerate([(0.0, 1.0), (1.0, ne15), (-15.0, eq15), (-1.0, ne0), (15.0, eq0)]):
         ts(ap("base", S(128 * i, 128 * i + 128)), v128, k, c, ALU.is_equal, ALU.mult)
@@ -317,85 +318,42 @@ def rank_body(g, core, T, topo, rank):
     ts(ap("jt", S(64, 128)), ap("jui"), 63, None, ALU.bitwise_and)
     ts(ap("xi"), ap("sti"), 63, None, ALU.bitwise_and)
     cp(ap("jb", S(0, 128)), ap("jt"))
+    cp(ap("fb0", S(0, PAD)), ap("fb0", S(PAD, LEAD)))
 
     def mat(name, i):
         return ap(name, S(128 * i, 128 * i + 128))
 
-    eye, mf, h64 = mat("base", 0), ap("mf"), ap("h64")
+    eye = mat("base", 0)
     for x in "AB":
         aset(ap("sq0" + x, allw, S(64, 80)), 16 * WMAX, 0.0)
     aset(ap("sq0A", S(0, 2), S(32, 48)), 32, 0.0)
-    act(ap("bp"), ap("base"), ACT.Identity, scale=0.5)
-    act(ap("bn"), ap("base"), ACT.Identity, scale=-0.5)
-    act(mat("i64", 0), eye, ACT.Identity, scale=64.0)
-    act(mat("i64", 1), eye, ACT.Identity, scale=-64.0)
-    act(mf, eye, ACT.Identity)
+    act(ap("nbase"), ap("base"), ACT.Identity, scale=-1.0)
+    for i, val in enumerate((1.0 / 64, 129.0, -129.0, 64.5, 129.0 / 128, 128.0, -128.0)):
+        act(mat("diag", i), eye, ACT.Identity, scale=val)
     aset(ap("mask0", S(1, 160, 10)), 16, big0)
     aset(ap("mask1", S(6, 160, 10)), 16, big15)
 
-    SIDE = (253.0 / 256, -127.0 / 256)
-    ts(ap("v0", S(0, 32)), ap("xi"), -1.0 / 128, None, ALU.mult)
+    SHRINK, SIDE = 128.0 / 129, (0.5 + 62.5 / 129, 0.5 / 129 - 0.5)
+    ts(ap("v0", S(0, 32)), ap("xi"), -1.0 / 129, None, ALU.mult)
     tt(ap("v0", S(64, 96)), ap("sti"), ap("jui", S(0, 32)), ALU.add)
     cp(ap("u16", 0, allc), ap("sti"))
     tt(ap("v0", S(32, 64)), ap("v0", S(0, 32)), ap("sti"), ALU.add)
     ts(ap("u16", 2, allc), ap("v0", S(64, 96)), 0.0, 4095.0, ALU.max, ALU.min)
-    ts(ap("ep", S(0, 128)), eye, 1.0, None, ALU.mult)
     ts(ap("u16", 1, allc), ap("v0", S(32, 64)), SIDE[0], None, ALU.add)
-    ts(h64, eye, 1.0 / 64, None, ALU.mult)
     for t in range(2):
         fill(ap("cq%d" % t, 2, allc), (32.5, 30.5)[t])
         fill(ap("mask%d" % t, S(4, 160, 5)), BIG)
         fill(ap("ce%d" % t, S(1, 5 * WMAX, 5)), -K2[t])
         fill(ap("ce%d" % t, S(2, 5 * WMAX, 5)), K2[t])
-        fill(ap("ce%d" % t, S(3, 5 * WMAX, 5)), 1952.0)
-        fill(ap("ce%d" % t, S(4, 5 * WMAX, 5)), 0.25)
+        fill(ap("ce%d" % t, S(3, 5 * WMAX, 5)), 30.5)
+        fill(ap("ce%d" % t, S(4, 5 * WMAX, 5)), 1.0 / 64)
+    fill(ap("mask1", S(0, 160, 5)), 0.0)
     fill(ap("mask0", S(2, 10, 5)), BIG)
     fill(ap("mask1", S(152, 160, 5)), BIG)
     fill(ap("floor", S(4, 5 * WMAX, 5)), BIG)
-    ts(ap("hp"), ap("base"), 127.0 / 128, None, ALU.mult)
-    ts(ap("hn"), ap("base"), -127.0 / 128, None, ALU.mult)
     ts(ap("tsel"), ap("vv", S(0, 144)), r16, 15.0, ALU.add, ALU.is_equal)
     for x in "AB":
         fill(ap("d" + x, 1, S(0, ND)), 0.0)
-
-    sent = 0
-    ms = split_mask(topo, core, rel[0], 4)
-    a = ap("jb", S(0, 128))
-    deps("g", [a], [])
-    g.remote_dma_fused([transfer(topo, core, rel[k], ms[k], T.sem.arrj, a[0], a[0]) for k in range(1, 4)],
-                       local_sem=T.sem.sent)
-    sent += sum(nbits(m) for m in ms[1:])
-    for h in range(2):
-        if h == 0:
-            gset(ap("sq1B", allw, S(0, 16)), 16 * WMAX, 0)
-        deps("g", [ap("fb0", S(4 * h * NP, 4 * (h + 1) * NP))], [])
-        trs = []
-        for k, c in enumerate(rel):
-            a = ap("fb0", S((4 * h + k) * NP, (4 * h + k + 1) * NP))
-            trs.append(transfer(topo, core, c, ms[k], T.sem["arr%d" % h], a[0], a[0]))
-        g.remote_dma_fused(trs, local_sem=T.sem.sent)
-        sent += sum(nbits(m) for m in ms)
-        if h == 0:
-            gset(ap("sq1B", allw, S(64, 80)), 16 * WMAX, 0)
-            gset(ap("sq1B", allw, S(32, 48)), 16 * WMAX, 0)
-
-    fs = [(rank + s) % n for s in range(n)]
-    w8 = 8 * WMAX
-    gset(ap("mask7"), 256, 0)
-    for nm in ("floor7", "dpf", "ce7"):
-        gset(ap(nm), w8, 0)
-    gset(ap("mask7", allc, 7), 32, BIG)
-    gset(ap("mask7", S(30, 32), 5), 2, BIG)
-    gset(ap("floor7", S(7, w8, 8)), WMAX, BIG)
-    for sl, val in ((0, fs[0] - fs[1]), (1, fs[1] - fs[2]), (2, fs[2] - fs[3]), (6, fs[3])):
-        gset(ap("dpf", S(sl, w8, 8)), WMAX, val)
-    for sl, val in ((4, -K2[1]), (5, K2[1]), (6, 2048)):
-        gset(ap("ce7", S(sl, w8, 8)), WMAX, val)
-
-    tiles = []
-    for s in range(8):
-        tiles.append((s, "A", 0, 2 * ROWS_A[s]))
-        tiles.append((s, "B", 2 * ROWS_A[s], 32))
 
     def exact(s, c0, c1):
         ts(ap("x16", S(3 * s, 3 * s + 3), S(c0, c1)), ap("u16", S(3 * s, 3 * s + 3), S(c0, c1)), -2048.0, None, ALU.add)
@@ -403,18 +361,63 @@ def rank_body(g, core, T, topo, rank):
     def rows_in(s, c0, c1):
         w = c1 - c0
         mm(ap("pq", S(0, 3), S(0, w)), eye, ap("cq%d" % (s % 2), S(0, 3), S(0, w)), start=True)
-        mm(ap("pq", S(0, 2), S(0, w)), mat("ep", 0), ap("x16", S(3 * s, 3 * s + 3, 2), S(c0, c1)))
-        mm(ap("pq", 2, S(0, w)), h64, ap("x16", 3 * s, S(c0, c1)), stop=True)
+        mm(ap("pq", S(0, 2), S(0, w)), eye, ap("x16", S(3 * s, 3 * s + 3, 2), S(c0, c1)))
+        mm(ap("pq", 2, S(0, w)), mat("diag", 0), ap("x16", 3 * s, S(c0, c1)), stop=True)
 
     def rows_out(s, c0, c1):
         act(ap("fl", S(3 * s, 3 * s + 3), S(c0, c1)), ap("pq", S(0, 3), S(0, c1 - c0)), ACT.Identity,
-            bias=192.0 - 4031.0 / 8192, scale=1.0 / 64)
+            bias=96.0 - 4031.0 / 16384, scale=1.0 / 128)
 
-    def steps(tile):
+    exact(0, 0, 32)
+
+    sent = 0
+    ms = split_mask(topo, core, rel[0], 4)
+    rows_in(0, 0, 32)
+    rows_out(0, 0, 32)
+    first = [ap("fb0", S(0, LEAD))] + 3 * [ap("jb", S(0, 128))]
+    deps("g", first, [])
+    g.remote_dma_fused([transfer(topo, core, rel[k], ms[k], T.sem.arrj, first[k][0], first[k][0]) for k in range(4)],
+                       local_sem=T.sem.sent)
+    sent += sum(nbits(m) for m in ms)
+    for h in range(2):
+        if h == 1:
+            act(ap("fb0", S(PAD + NF, NB)), ap("fb0", S(NF, PAD + NF)), ACT.Copy)
+        deps("g", [ap("fb0", S(LEAD + 4 * h * NP, LEAD + 4 * (h + 1) * NP))], [])
+        trs = []
+        for k, c in enumerate(rel):
+            a = ap("fb0", S(LEAD + (4 * h + k) * NP, LEAD + (4 * h + k + 1) * NP))
+            trs.append(transfer(topo, core, c, ms[k], T.sem["arr%d" % h], a[0], a[0]))
+        g.remote_dma_fused(trs, local_sem=T.sem.sent)
+        sent += sum(nbits(m) for m in ms)
+    for lo in (0, 64, 32):
+        gset(ap("sq1B", allw, S(lo, lo + 16)), 16 * WMAX, 0)
+
+    fs = [(rank + s) % n for s in range(n)]
+    w8 = 8 * WMAX
+    gset(ap("mask7"), 256, 0)
+    gset(ap("floor7"), w8, -BIG)
+    for nm in ("dpf", "ce7"):
+        gset(ap(nm), w8, 0)
+    gset(ap("mask7", allc, S(4, 7)), 96, -OFF)
+    gset(ap("mask7", allc, 7), 32, BIG)
+    gset(ap("mask7", S(30, 32), 5), 2, BIG)
+    gset(ap("floor7", S(7, w8, 8)), WMAX, BIG)
+    for sl, val in ((0, fs[0] - fs[1]), (1, fs[1] - fs[2]), (2, fs[2] - fs[3]), (6, fs[3])):
+        gset(ap("dpf", S(sl, w8, 8)), WMAX, val)
+    for sl, val in ((4, -64 * K2[1]), (5, 64 * K2[1]), (6, 2048)):
+        gset(ap("ce7", S(sl, w8, 8)), WMAX, val)
+
+    tiles = []
+    for s in range(8):
+        tiles.append((s, "A", 0, 2 * ROWS_A[s]))
+        tiles.append((s, "B", 2 * ROWS_A[s], 32))
+    if OPT["split"]:
+        tiles[15:] = [(7, "B", 2 * ROWS_A[7], 32 - OPT["split"]), (7, "A", 32 - OPT["split"], 32)]
+
+    def steps(tile, part):
         s, x, c0, c1 = tile
         w, t = c1 - c0, s % 2
         ns, o = (8, 3) if s == 7 else (5, 0)
-        pos, neg = ("ep", "en") if s == 7 else ("hp", "hn")
         sh, wr, dc = (1, 2, -2) if t == 0 else (3, 4, 2)
         b0, b1 = max(c0, -dc), min(c1, 32 - dc)
         here, vert = (c0, c1, 1, 0), (b0, b1, 1, dc)
@@ -438,32 +441,35 @@ def rank_body(g, core, T, topo, rank):
                     first = ns * (a0 - c0) + slot
                     calls.append((ap("pe" + x, S(first, first + ns * st * (cnt - 1) + 1, ns * st)), lhs, rhs))
 
-        for k, m, row, span in xt:
-            add(k, mat(pos, m), mat(neg, m), "x16", row, span)
-        for k, m, row, span in ft:
-            add(k, mat("bp", m), mat("bn", m), "fl", row, span)
-        add(o + 2, mat("i64", 1), mat("i64", 0), "fl", 3 * s + 2, vert)
-        mm(ap("pe" + x, S(0, ns * w)), eye, ap("ce7" if s == 7 else "ce%d" % t, S(0, ns * w)), start=True)
+        if part == 0:
+            for k, m, row, span in xt:
+                add(k, mat("base", m), mat("nbase", m), "x16", row, span)
+            mm(ap("pe" + x, S(0, ns * w)), eye if s == 7 else mat("diag", 3),
+               ap("ce7" if s == 7 else "ce%d" % t, S(0, ns * w)), start=True)
+        else:
+            for k, m, row, span in ft:
+                add(k, mat("base", m), mat("nbase", m), "fl", row, span)
+            add(o + 2, mat("diag", 6 if s == 7 else 2), mat("diag", 5 if s == 7 else 1), "fl", 3 * s + 2, vert)
         for i, c in enumerate(calls):
-            mm(c[0], c[1], c[2], stop=(s == 7 and i == len(calls) - 1))
+            mm(c[0], c[1], c[2], stop=(s == 7 and part == 1 and i == len(calls) - 1))
 
     def jumps(tile):
         s, x, c0, c1 = tile
         if s < 7:
             j = 128 * ((s + 1) // 2) + 32 * (1 - s % 2)
             out = ap("pe" + x, S(4, 5 * (c1 - c0), 5))
-            mm(out, mat("i64", 0), ap("jb", S(j + c0, j + c1)))
-            mm(out, eye, ap("jb", S(j + 64 + c0, j + 64 + c1)), stop=True)
+            mm(out, mat("diag", 3), ap("jb", S(j + c0, j + c1)))
+            mm(out, mat("diag", 4), ap("jb", S(j + 64 + c0, j + 64 + c1)), stop=True)
 
-    def gather(tile, k, u0=0):
+    def gather(tile, k, u0, u1):
         s, x, c0, c1 = tile
         t, fb = s % 2, "fb%d" % (s // 2)
-        a0, a1, row, base, sh, dc = c0 + u0, c1, 0, PAD, 0, 0
+        a0, a1, row, base, sh, dc = c0 + u0, c0 + u1, 0, PAD, 0, 0
         if k == 1:
             row, sh = 1, 1 - 2 * t
         if k == 2:
             dc = -2 if t == 0 else 2
-            a0, a1, base = max(c0, -dc), min(c1, 32 - dc), PAD * (2 - 2 * t)
+            a0, a1, base = max(a0, -dc), min(a1, 32 - dc), PAD * (2 - 2 * t)
         if k == 3:
             row = 2
         m, o = 16 * (a1 - a0), 16 + 16 * (a0 - c0)
@@ -506,11 +512,11 @@ def rank_body(g, core, T, topo, rank):
         if s == 7:
             mm(ap("p7" + x, S(0, w), S(0, 8)), eye, ap("mask7", S(c0, c1), S(0, 8)), start=True)
             for j, sj in enumerate((1, 3, 5, 6)):
-                mm(ap("p7" + x, S(0, w), j), mf, least(sj, c0, c1))
+                mm(ap("p7" + x, S(0, w), j), eye, least(sj, c0, c1))
         else:
             mm(ap("ps" + x, S(0, 5 * w)), eye, ap("mask%d" % (s % 2), S(5 * c0, 5 * c1)), start=True)
             if s % 2:
-                mm(ap("ps" + x, S(0, 5 * w, 5)), mf, least(s - 1, c0, c1))
+                mm(ap("ps" + x, S(0, 5 * w, 5)), eye, least(s - 1, c0, c1))
 
     def sums(tile):
         s, x, c0, c1 = tile
@@ -537,7 +543,7 @@ def rank_body(g, core, T, topo, rank):
         def two():
             tt(ni, ps, ap(mb, S(mo, mo + m)), ALU.is_ge)
             if s == 7:
-                act(ap("oc", S(c0, c1)), ap(mb, S(mo + 7, mo + m, 8)), ACT.Copy)
+                act(ap("oc", S(c0, c1)), ap(mb, S(mo + 7, mo + m, 8)), ACT.Identity, bias=OFF)
 
         def three():
             scan(z, ni, ap("pe" + x, S(0, m)), 0.0, ALU.mult, ALU.add)
@@ -550,52 +556,60 @@ def rank_body(g, core, T, topo, rank):
                 cp(ap("of", S(c0, c1)), ap("zf" + x, S(6, m, 8)))
                 return
             v, r = ap("z" + x, S(3, m, 5)), 3 * (s + 1)
-            ts(ap("u16", r + 2, S(c0, c1)), ap("z" + x, S(4, m, 5)), 0.0, 4095.0, ALU.max, ALU.min)
-            ts(ap("u16", r, S(c0, c1)), v, 0.25, None, ALU.add)
-            ts(ap("u16", r + 1, S(c0, c1)), v, SIDE[(s + 1) % 2], None, ALU.add)
+            ts(ap("u16", r, S(c0, c1)), v, SHRINK, 0.75 * SHRINK + 0.25, ALU.mult, ALU.add)
+            ts(ap("u16", r + 2, S(c0, c1)), ap("z" + x, S(4, m, 5)), SHRINK, 4095.0, ALU.mult, ALU.min)
+            ts(ap("u16", r + 1, S(c0, c1)), v, SHRINK, 0.75 * SHRINK + SIDE[(s + 1) % 2], ALU.mult, ALU.add)
 
         return [one, two, three, four]
 
-    exact(0, 0, 32)
-    rows_in(0, 0, 32)
-    rows_out(0, 0, 32)
     nt = len(tiles)
     for i in range(nt + 1):
         tile = tiles[i] if i < nt else None
         prev = tiles[i - 1] if i >= 1 else None
-        made = tiles[i - 2] if 2 <= i < nt else None
+        made = tiles[i - 2] if 2 <= i < 16 else None
         todo = pick(prev) if prev else []
         if tile:
             t, u = tile[0] % 2, side_cols(tile)
-            order = [(2, 0)] + ([(0, 0)] if t == 0 else []) + [(1, 0)] + ([(3, u)] if u < tile[3] - tile[2] else [])
-            late = OPT["after"][t] if prev else 0
-            if u:
-                side_gather(tile)
-            if prev:
-                sums(prev)
-                jumps(prev)
-            if u:
-                side_diff(tile)
-            for j, (k, u0) in enumerate(order):
-                if j >= len(order) - late:
+            w = tile[3] - tile[2]
+            order = [(2, 0, w), (1, 0, w)] + ([(0, 0, w)] if t == 0 else []) + ([(3, u, w)] if u < w else [])
+            if i == 0:
+                order.append(order.pop(0))
+            cut = order[-1][2] - OPT["cut"][t]
+            if OPT["cut"][t] and cut > order[-1][1]:
+                order[-1:] = [(order[-1][0], order[-1][1], cut), (order[-1][0], cut, w)]
+            if i == nt - 4:
+                aset(ap("mask7", S(1, 32, 2), 4), 16, big15)
+            for c in OPT["last"] if i == nt - 1 else OPT["plan"][t]:
+                if c == "g" and order:
+                    gather(tile, *order.pop(0))
+                if c == "G":
+                    while order:
+                        gather(tile, *order.pop(0))
+                if c == "p" and todo:
                     todo.pop(0)()
-                gather(tile, k, u0)
-                if j == 0:
-                    if made:
-                        exact(tile[0], made[2], made[3])
-                        rows_in(tile[0], made[2], made[3])
-                    if u:
-                        side_square(tile)
-                    if i == nt - 3:
-                        ts(ap("ep", S(128, 640)), ap("base", S(128, 640)), 1.0, None, ALU.mult)
-                        ts(ap("en"), ap("base"), -1.0, None, ALU.mult)
-                        aset(ap("mask7", S(1, 32, 2), 4), 16, big15)
+                if c == "a" and u:
+                    side_gather(tile)
+                if c == "d" and u:
+                    side_diff(tile)
+                if c == "q" and u:
+                    side_square(tile)
+                if c == "s" and prev:
+                    sums(prev)
+                if c == "f" and prev:
+                    steps(prev, 1)
+                    jumps(prev)
+                if c == "x" and made:
+                    exact(tile[0], made[2], made[3])
+                if c == "r" and made:
+                    rows_in(tile[0], made[2], made[3])
+                if c == "o" and made:
+                    rows_out(tile[0], made[2], made[3])
+                if c == "m":
                     sums_pre(tile)
-                if j == 1:
-                    if made:
-                        rows_out(tile[0], made[2], made[3])
-                    steps(tile)
+                if c == "e":
+                    steps(tile, 0)
         else:
+            steps(prev, 1)
             sums(prev)
         for f in todo:
             f()

@@ -5,45 +5,55 @@ from concourse.mybir import AluOpType, ActivationFunctionType
 NF = 4096
 PAD = 64
 NB = NF + 2 * PAD
-LEAD = 2 * PAD
-NP = (NB - LEAD) // 8
+LEAD = 128
+NP = (NF - 4 * LEAD) // 8
+SUB = 2
 BIG = 8192.0
 OFF = 2048.0
 OPT = {
-    "rows0": 10,
-    "side": [20, 14],
+    "rows0": (8, 13),
+    "g": (0.1, 0.3, 0.5, 0.7),
+    "p": (0.0, 0.2, 0.4, 0.9),
+    "x": (0.6, 0.15, 0.6, 0.15),
+    "end": (0.1, 0.3, 0.5, 0.15, 1.0),
+    "side": [20, 6],
     "last": "asgxrdfomegqG",
-    "plan": ["asgdfgqpxrgpmeGpop", "asgdfgqpxrgpmeGpop"],
+    "first": "aAsgdfgqDmeGQc",
+    "plan": ["aAsdfgqDgxprgmGpQppeo", "sagdqgpfgxrpoeGpmp"],
     "cut": [0, 0],
+    "more": [0, 0],
+    "order": [(2, 1, 0, 3), (2, 1, 3)],
     "split": 0,
 }
-ROWS_A = [OPT["rows0"] - (s + 1) // 2 for s in range(8)]
-WMAX = max(max(2 * r, 32 - 2 * r) for r in ROWS_A)
+BOUNDS = [[0] + [2 * (r - (s + 1) // 2) for r in OPT["rows0"]] + [32] for s in range(8)]
+WMAX = max(b[j + 1] - b[j] for b in BOUNDS for j in range(3))
+CYCLE, CALL, WAKE, LOOKUP, SLACK = 0.00083, 0.05, 0.2, 1.56, 0.03
 ND = 16 * WMAX + 32
 NM = 164
 
 SCRATCH = {
     "jb": ("sbuf", [128, 512], "bfloat16"),
     "q": ("sbuf", [128, 544], "bfloat16"),
-    "gs": ("sbuf", [128, 16 * WMAX], "bfloat16"),
+    "gs": ("sbuf", [128, 2, 16 * WMAX], "bfloat16"),
     "sti": ("sbuf", [128, 32], "int32"),
     "jui": ("sbuf", [128, 64], "int32"),
     "jt": ("sbuf", [128, 128], "int32"),
     "xi": ("sbuf", [128, 32], "int32"),
     "v0": ("sbuf", [128, 96], "float32"),
-    "vv": ("sbuf", [128, 320], "bfloat16"),
+    "vv": ("sbuf", [128, 144], "bfloat16"),
     "pi": ("sbuf", [128, 8], "int32"),
     "col": ("sbuf", [128, 8], "float32"),
     "tsel": ("sbuf", [128, 144], "bfloat16"),
     "base": ("sbuf", [128, 640], "bfloat16"),
     "nbase": ("sbuf", [128, 640], "bfloat16"),
+    "wide": ("sbuf", [128, 1024], "bfloat16"),
     "diag": ("sbuf", [128, 896], "bfloat16"),
     "mask0": ("sbuf", [128, 160], "bfloat16"),
     "mask1": ("sbuf", [128, 160], "bfloat16"),
     "mask7": ("sbuf", [128, 32, 8], "bfloat16"),
-    "ce0": ("sbuf", [128, 5 * WMAX], "bfloat16"),
-    "ce1": ("sbuf", [128, 5 * WMAX], "bfloat16"),
-    "ce7": ("sbuf", [128, 8 * WMAX], "bfloat16"),
+    "ce0": ("sbuf", [128, 120], "float16"),
+    "ce1": ("sbuf", [128, 120], "float16"),
+    "ce7": ("sbuf", [128, 192], "bfloat16"),
     "cq0": ("sbuf", [128, 3, 32], "bfloat16"),
     "cq1": ("sbuf", [128, 3, 32], "bfloat16"),
     "floor": ("sbuf", [128, 5 * WMAX], "float32"),
@@ -73,7 +83,7 @@ for _x in "AB":
     SCRATCH["pe" + _x] = ("psum", [128, 512], "float32")
     SCRATCH["p7" + _x] = ("psum", [128, 64, 8], "float32")
 
-SEMAPHORES = ["sv", "sa", "sp", "sq", "ld0", "ld1", "lp", "lj", "ls", "lq", "sent", "arrj", "arr0", "arr1",
+SEMAPHORES = ["sv", "sa", "sp", "sq", "ld0", "ld1", "lp", "lj", "ls", "lq", "sent", "arrl", "arrj", "arr0", "arr1", "arr2", "arr3",
               "fj1", "fj2", "fj3", "fa1", "fa2", "fa3", "out0", "out1", "out2"]
 
 
@@ -106,38 +116,49 @@ def transfer(topo, src, dst, mask, sem, a, b):
     return RemoteDMATransfer(dst_ids=[DstId(rid=rid, pnc=pid)], dma_engine_mask=mask, remote_sem=sem, src=a, dst=b)
 
 
+def lead_cols(k):
+    return slice(PAD + k * LEAD, PAD + (k + 1) * LEAD)
+
+
+def piece_cols(k, h):
+    lo = PAD + 4 * LEAD + (4 * h + k) * NP
+    return slice(lo, lo + NP)
+
+
+def part_cols(k, j):
+    lo = piece_cols(k, j // SUB).start + (j % SUB) * NP // SUB
+    return slice(lo, lo + NP // SUB)
+
+
 def relay_program(g, core, T, topo, src, k):
     n = len(T.cores)
     r = T.rank_of(src)
-    cols = [slice(LEAD + (4 * h + k) * NP, LEAD + (4 * h + k + 1) * NP) for h in range(2)]
     got = nbits(split_mask(topo, src, core, 4)[k])
-    total = 0
-    g.wait_ge(T.sem.arrj, got)
-    if k >= 1:
-        d = T.cores[(r - k) % n]
-        rid, pid = topo.addr(d, core)
-        m = topo.mask(core, d)
-        g.remote_dma(T.jb[:, 128 * k:128 * k + 128], T.jb[:, 0:128], T.sem["fj%d" % k], T.sem.sent, pid, rid, m)
-        total += nbits(m)
-    for step in range(1, n):
+    total = [0]
+
+    def send(step, name, dst, a, sem):
         d = T.cores[(r - step) % n]
         rid, pid = topo.addr(d, core)
         m = topo.mask(core, d)
-        sem = T.sem["fa%d" % step]
-        if k == 0:
-            g.remote_dma(T["fb%d" % step][:, 0:LEAD], T.fb0[:, 0:LEAD], sem, T.sem.sent, pid, rid, m)
-            total += nbits(m)
-        if step == 1:
-            for h in range(2):
-                g.wait_ge(T.sem["arr%d" % h], got)
-                g.remote_dma(T.fb1[:, cols[h]], T.fb0[:, cols[h]], sem, T.sem.sent, pid, rid, m)
-                total += nbits(m)
-        else:
-            ms = split_mask(topo, core, d, 2)
-            g.remote_dma_fused([transfer(topo, core, d, ms[h], sem, T.fb0[:, cols[h]], T["fb%d" % step][:, cols[h]])
-                                for h in range(2)], local_sem=T.sem.sent)
-            total += nbits(m)
-    g.wait_ge(T.sem.sent, total)
+        g.remote_dma(T[name][:, dst], a, T.sem[sem], T.sem.sent, pid, rid, m)
+        total[0] += nbits(m)
+
+    g.wait_ge(T.sem.arrl, got)
+    send(1, "fb1", lead_cols(k), T.fb0[:, lead_cols(k)], "fa1")
+    if k >= 1:
+        g.wait_ge(T.sem.arrj, got)
+        send(k, "jb", slice(128 * k, 128 * k + 128), T.jb[:, 0:128], "fj%d" % k)
+    for j in range(2 * SUB):
+        g.wait_ge(T.sem["arr%d" % j], got)
+        send(1, "fb1", part_cols(k, j), T.fb0[:, part_cols(k, j)], "fa1")
+    for step in range(2, n):
+        d = T.cores[(r - step) % n]
+        ms = split_mask(topo, core, d, 2)
+        send(step, "fb%d" % step, lead_cols(k), T.fb0[:, lead_cols(k)], "fa%d" % step)
+        g.remote_dma_fused([transfer(topo, core, d, ms[h], T.sem["fa%d" % step], T.fb0[:, piece_cols(k, h)],
+                                     T["fb%d" % step][:, piece_cols(k, h)]) for h in range(2)], local_sem=T.sem.sent)
+        total[0] += sum(nbits(m) for m in ms)
+    g.wait_ge(T.sem.sent, total[0])
 
 
 def make_emitter(g, T):
@@ -147,6 +168,8 @@ def make_emitter(g, T):
     known = {q: {} for q in queues}
     hist = {}
     grids = {}
+    held = []
+    place = [0.0]
 
     def ap(name, *idx):
         if name not in grids:
@@ -159,7 +182,7 @@ def make_emitter(g, T):
             flags = np.zeros(grids[name].size, np.uint8)
             flags[grids[name][tuple(idx)].reshape(-1) if idx else slice(None)] = 1
             bits = int.from_bytes(np.packbits(flags, bitorder="little").tobytes(), "little")
-        return (T[name][full], name, bits)
+        return (T[name][full], name, bits, int(grids[name][tuple(idx)].size if idx else grids[name].size))
 
     def wait(q, ev):
         sem, val, clock = ev
@@ -198,7 +221,13 @@ def make_emitter(g, T):
         for ev in best.values():
             wait(q, ev)
 
-    def op(q, fn, reads, writes):
+    def op(q, fn, reads, writes, cost=0.0):
+        if held:
+            if q == "p":
+                held[-1].append((q, fn, reads, writes, cost))
+            else:
+                held.extend([[(q, fn, reads, writes, cost, (place[0], len(held)))], []])
+            return None
         deps(q, reads, writes)
         sem = own[q]
         count[sem] += 1
@@ -224,42 +253,100 @@ def make_emitter(g, T):
         for ev in evs:
             wait(q, ev)
 
-    return ap, op, dma, landed, deps, finish
+    def task(fn, *args):
+        held.append([])
+        fn(*args)
+
+    def flush():
+        tasks = [t for t in held if t]
+        del held[:]
+        seen, before, after = {}, [], [[] for t in tasks]
+        for i, t in enumerate(tasks):
+            need = set()
+            for c in t:
+                for a, wr in [(a, False) for a in c[2]] + [(a, True) for a in c[3]]:
+                    wr = wr or SCRATCH[a[1]][0] == "psum"
+                    need.update(j for j, bits, w in seen.get(a[1], []) if bits & a[2] and (w or wr) and j != i)
+            for c in t:
+                for a in c[3]:
+                    seen[a[1]] = [e for e in seen.get(a[1], []) if e[1] & ~a[2]] + [(i, a[2], True)]
+                for a in c[2]:
+                    seen.setdefault(a[1], []).append((i, a[2], SCRATCH[a[1]][0] == "psum"))
+            before.append(need)
+            for j in need:
+                after[j].append(i)
+        row = sorted((i for i, t in enumerate(tasks) if t[0][0] == "v"), key=lambda i: tasks[i][0][5])
+        free_of = set()
+        for j, i in zip(row, row[1:]):
+            if j not in before[i]:
+                before[i].add(j)
+                after[j].append(i)
+                free_of.add((j, i))
+        span = [sum(c[4] for c in t) for t in tasks]
+        lag = lambda j, i: 0.0 if tasks[j][0][0] == tasks[i][0][0] == "p" or (j, i) in free_of else WAKE
+        way = list(span)
+        chain, cnt = [i for i in range(len(tasks)) if not before[i]], [len(b) for b in before]
+        for i in chain:
+            for j in after[i]:
+                cnt[j] -= 1
+                if not cnt[j]:
+                    chain.append(j)
+        for i in reversed(chain):
+            way[i] += max([lag(i, j) + way[j] for j in after[i]], default=0.0)
+        left, end, free = [len(b) for b in before], {}, {q: 0.0 for q in queues}
+        ready = [i for i in range(len(tasks)) if not left[i]]
+        while ready:
+            start = {i: max([free[tasks[i][0][0]]] + [end[j] + lag(j, i) for j in before[i]]) for i in ready}
+            soon = min(start.values())
+            i = max((i for i in ready if start[i] <= soon + SLACK), key=lambda i: way[i])
+            ready.remove(i)
+            end[i] = free[tasks[i][0][0]] = start[i] + span[i]
+            for c in tasks[i]:
+                op(*c[:4])
+            for j in after[i]:
+                left[j] -= 1
+                if not left[j]:
+                    ready.append(j)
+
+    return ap, op, dma, landed, deps, finish, task, flush, place
 
 
 def rank_body(g, core, T, topo, rank):
     n = len(T.cores)
     ALU, ACT = AluOpType, ActivationFunctionType
-    ap, op, dma, landed, deps, finish = make_emitter(g, T)
+    ap, op, dma, landed, deps, finish, task, flush, place = make_emitter(g, T)
     S = slice
+
+    def small(out):
+        return max(64, out[3]) * CYCLE
 
     def ts(out, in0, s1, s2, o0, o1=None):
         a1 = s1[0] if isinstance(s1, tuple) else s1
         a2 = s2[0] if isinstance(s2, tuple) else s2
         rd = [in0] + [s for s in (s1, s2) if isinstance(s, tuple)]
         if o1 is None:
-            return op("v", lambda e: e.tensor_scalar(out[0], in0[0], a1, None, o0), rd, [out])
-        return op("v", lambda e: e.tensor_scalar(out[0], in0[0], a1, a2, o0, o1), rd, [out])
+            return op("v", lambda e: e.tensor_scalar(out[0], in0[0], a1, None, o0), rd, [out], small(out))
+        return op("v", lambda e: e.tensor_scalar(out[0], in0[0], a1, a2, o0, o1), rd, [out], small(out))
 
     def tt(out, in0, in1, o):
-        return op("v", lambda e: e.tensor_tensor(out[0], in0[0], in1[0], o), [in0, in1], [out])
+        return op("v", lambda e: e.tensor_tensor(out[0], in0[0], in1[0], o), [in0, in1], [out], small(out))
 
     def cp(out, in0):
-        return op("v", lambda e: e.tensor_copy(out[0], in0[0]), [in0], [out])
+        return op("v", lambda e: e.tensor_copy(out[0], in0[0]), [in0], [out], small(out))
 
     def fill(out, val):
-        return op("v", lambda e: e.memset(out[0], val), [], [out])
+        return op("v", lambda e: e.memset(out[0], val), [], [out], small(out))
 
     def scan(out, d0, d1, init, o0, o1):
-        return op("v", lambda e: e.tensor_tensor_scan(out[0], d0[0], d1[0], init, o0, o1), [d0, d1], [out])
+        return op("v", lambda e: e.tensor_tensor_scan(out[0], d0[0], d1[0], init, o0, o1), [d0, d1], [out], small(out))
 
     def act(out, in0, func, bias=0.0, scale=1.0):
         b = bias[0] if isinstance(bias, tuple) else bias
         rd = [in0] + ([bias] if isinstance(bias, tuple) else [])
-        return op("a", lambda e: e.activation(out[0], in0[0], func, bias=b, scale=scale), rd, [out])
+        return op("a", lambda e: e.activation(out[0], in0[0], func, bias=b, scale=scale), rd, [out], CALL + small(out))
 
     def mm(out, lhs, rhs, start=False, stop=False):
-        return op("p", lambda e: e.matmul(out[0], lhs[0], rhs[0], start, stop), [lhs, rhs], [out])
+        return op("p", lambda e: e.matmul(out[0], lhs[0], rhs[0], start, stop), [lhs, rhs], [out], small(out) / 2)
 
     def aset(out, cnt, val):
         act(out, ap("vv", S(0, cnt)), ACT.Identity, bias=val, scale=0.0)
@@ -270,38 +357,58 @@ def rank_body(g, core, T, topo, rank):
     allc, allw = S(0, 32), S(0, WMAX)
     rel = relays_of(T, topo, core)
 
-    a = ap("jui"); dma("s", a[0], T.ju[:], "lj", [], [a])
+    sent = [0]
+
+    def hand(parts, sem):
+        ms = split_mask(topo, core, rel[0], 4)
+        ks = [k for k in range(4) if parts[k]]
+        deps("g", [parts[k] for k in ks], [])
+        g.remote_dma_fused([transfer(topo, core, rel[k], ms[k], T.sem[sem], parts[k][0], parts[k][0]) for k in ks],
+                           local_sem=T.sem.sent)
+        sent[0] += sum(nbits(ms[k]) for k in ks)
+
+    def borders(step):
+        for e0, r0 in ((PAD + NF, NF), (0, PAD)):
+            edge, row = ap("fb%d" % step, S(e0, e0 + PAD)), ap("fb%d" % step, S(r0, r0 + PAD))
+            op("g", lambda e: e.affine_select(edge[0], row[0], [[0, PAD]], ALU.is_ge, 0.0, 0, 0), [row], [edge])
+
+    a = ap("fb0", S(PAD, PAD + 4 * LEAD)); dma("s", a[0], T.fr[:, 0:4 * LEAD], "lp", [], [a])
+    a = ap("jui"); dma("a", a[0], T.ju[:], "lj", [], [a])
     a = ap("sti"); dma("a", a[0], T.st[:], "ls", [], [a])
-    a = ap("fb0", S(PAD, LEAD)); dma("a", a[0], T.fr[:, 0:PAD], "lp", [], [a])
     a = ap("q", S(16, 528)); dma("a", a[0], T.qu[:], "lq", [], [a])
     for h in range(2):
-        lo, hi = LEAD + 4 * h * NP, min(LEAD + 4 * (h + 1) * NP, PAD + NF)
+        lo, hi = piece_cols(0, h).start, piece_cols(3, h).stop
         a = ap("fb0", S(lo, hi)); dma("s", a[0], T.fr[:, lo - PAD:hi - PAD], "ld%d" % h, [], [a])
     for step in range(1, n):
         far = relays_of(T, topo, T.cores[(rank + step) % n])
         landed(ap("jb", S(128 * step, 128 * step + 128)), "fj%d" % step, nbits(topo.mask(far[step], core)))
-        landed(ap("fb%d" % step), "fa%d" % step, (9 if step == 1 else 5) * nbits(topo.mask(far[0], core)))
+        landed(ap("fb%d" % step, S(PAD, PAD + NF)), "fa%d" % step,
+               (1 + 2 * SUB if step == 1 else 2) * sum(nbits(topo.mask(c, core)) for c in far))
 
     a2 = ap("pi", S(0, 1))
     op("g", lambda e: e.iota(a2[0], [[1, 1]], 0, 1), [], [a2])
     a3 = ap("vv")
-    op("g", lambda e: e.iota(a3[0], [[1, 320]], 0, -1, allow_small_or_imprecise_dtypes=True), [], [a3])
-    gset(ap("sq1A", allw, S(0, 16)), 16 * WMAX, 0)
-    gset(ap("sq1A", allw, S(64, 80)), 16 * WMAX, 0)
+    op("g", lambda e: e.iota(a3[0], [[1, 144]], 0, -1, allow_small_or_imprecise_dtypes=True), [], [a3])
 
-    K2 = (193.0, 191.0)
-    for t in range(2):
-        fill(ap("mask%d" % t), -OFF)
-        fill(ap("ce%d" % t), 0.0)
-        fill(ap("cq%d" % t), 0.0)
+    K2 = (195.0, 193.0)
+    w5 = 5 * WMAX
+    fill(ap("mask0"), -OFF)
+    fill(ap("ce0"), 0.0)
+    fill(ap("cq0"), 0.0)
     fill(ap("floor"), -BIG)
     ts(ap("pi", S(4, 5)), ap("pi", S(0, 1)), 15, None, ALU.bitwise_and)
-    fill(ap("mc", S(0, 7 * NM, NM)), BIG)
-    fill(ap("m7", S(0, 1)), BIG)
+    fill(ap("sq0A", allw, S(64, 80)), 0.0)
     r16 = ap("col", S(0, 1))
     cp(r16, ap("pi", S(4, 5)))
-    fill(ap("q", S(0, 16)), 0.0)
-    fill(ap("q", S(528, 544)), 0.0)
+    fill(ap("sq0B", allw, S(64, 80)), 0.0)
+    for a, cnt, val in ((ap("q", S(0, 16)), 16, 0), (ap("q", S(528, 544)), 16, 0), (ap("sq0B", S(0, 2), S(32, 48)), 32, 0),
+                        (ap("mask0", S(2, 10, 5)), 2, BIG), (ap("floor", S(4, w5, 5)), WMAX, BIG)):
+        gset(a, cnt, val)
+    hand([ap("fb0", lead_cols(k)) for k in range(4)], "arrl")
+    for a, cnt, val in ((ap("sq0A", S(0, 2), S(32, 48)), 32, 0.0), (ap("cq0", 2, allc), 32, 32.5),
+                        (ap("dA", 1, S(16, 17)), 1, 0.0), (ap("dB", 1, S(16, 17)), 1, 0.0),
+                        (ap("dB", 1, S(176, ND)), ND - 176, 0.0), (ap("mask0", S(4, 160, 5)), 32, BIG)):
+        aset(a, cnt, val)
     ne15, ne0, eq15, eq0, big15, big0 = [ap("col", S(i, i + 1)) for i in range(1, 7)]
     ts(ne15, r16, 15.0, None, ALU.not_equal)
     ts(eq15, r16, 15.0, None, ALU.is_equal)
@@ -310,50 +417,55 @@ def rank_body(g, core, T, topo, rank):
     ts(eq0, r16, 0.0, None, ALU.is_equal)
     ts(big15, r16, 15.0, BIG, ALU.is_equal, ALU.mult)
     ts(ap("col", S(5, 7)), ap("col", S(5, 7)), -OFF, None, ALU.add)
+
     v128 = ap("vv", S(0, 128))
     for i, (k, c) in enumerate([(0.0, 1.0), (1.0, ne15), (-15.0, eq15), (-1.0, ne0), (15.0, eq0)]):
         ts(ap("base", S(128 * i, 128 * i + 128)), v128, k, c, ALU.is_equal, ALU.mult)
-
-    ts(ap("jt", S(0, 64)), ap("jui"), 6, None, ALU.arith_shift_right)
-    ts(ap("jt", S(64, 128)), ap("jui"), 63, None, ALU.bitwise_and)
-    ts(ap("xi"), ap("sti"), 63, None, ALU.bitwise_and)
-    cp(ap("jb", S(0, 128)), ap("jt"))
-    cp(ap("fb0", S(0, PAD)), ap("fb0", S(PAD, LEAD)))
 
     def mat(name, i):
         return ap(name, S(128 * i, 128 * i + 128))
 
     eye = mat("base", 0)
-    for x in "AB":
-        aset(ap("sq0" + x, allw, S(64, 80)), 16 * WMAX, 0.0)
-    aset(ap("sq0A", S(0, 2), S(32, 48)), 32, 0.0)
-    act(ap("nbase"), ap("base"), ACT.Identity, scale=-1.0)
-    for i, val in enumerate((1.0 / 64, 129.0, -129.0, 64.5, 129.0 / 128, 128.0, -128.0)):
+    act(mat("nbase", 0), eye, ACT.Identity, scale=-1.0)
+    for i, val in enumerate((1.0 / 64, 129.0, -129.0, 64.5, 129.0 / 128)):
         act(mat("diag", i), eye, ACT.Identity, scale=val)
+
+    def last_sweep_matrices():
+        act(ap("nbase", S(384, 640)), ap("base", S(384, 640)), ACT.Identity, scale=-1.0)
+        act(mat("diag", 5), eye, ACT.Identity, scale=128.0)
+        act(mat("diag", 6), eye, ACT.Identity, scale=-128.0)
+
     aset(ap("mask0", S(1, 160, 10)), 16, big0)
-    aset(ap("mask1", S(6, 160, 10)), 16, big15)
+    ts(ap("tsel"), ap("vv", S(0, 144)), r16, 15.0, ALU.add, ALU.is_equal)
+    for sl, val in enumerate((-1.5, 1.5 - K2[0], K2[0], 30.5)):
+        fill(ap("ce0", S(sl, 120, 5)), val)
+    act(ap("wide", S(0, 256)), ap("base", S(128, 384)), ACT.Identity, scale=129.0 / 128)
+    act(ap("wide", S(512, 768)), ap("base", S(128, 384)), ACT.Identity, scale=-129.0 / 128)
+
+    def second_sweep_constants():
+        fill(ap("mask1"), -OFF)
+        cp(ap("ce1"), ap("ce0"))
+        fill(ap("cq1"), 0.0)
+        fill(ap("m7", S(0, 1)), BIG)
+        fill(ap("mask1", S(4, 160, 5)), BIG)
+        fill(ap("ce1", S(1, 120, 5)), 1.5 - K2[1])
+        fill(ap("ce1", S(2, 120, 5)), K2[1])
+        fill(ap("cq1", 2, allc), 30.5)
+        fill(ap("mask1", S(0, 160, 5)), 0.0)
+        fill(ap("mask1", S(152, 160, 5)), BIG)
+        ts(ap("mask1", S(6, 160, 10)), ap("vv", S(0, 16)), 0.0, big15, ALU.mult, ALU.add)
 
     SHRINK, SIDE = 128.0 / 129, (0.5 + 62.5 / 129, 0.5 / 129 - 0.5)
+    ts(ap("jt", S(0, 64)), ap("jui"), 6, None, ALU.arith_shift_right)
+    ts(ap("jt", S(64, 128)), ap("jui"), 63, None, ALU.bitwise_and)
+    ts(ap("xi"), ap("sti"), 63, None, ALU.bitwise_and)
+    cp(ap("jb", S(0, 128)), ap("jt"))
     ts(ap("v0", S(0, 32)), ap("xi"), -1.0 / 129, None, ALU.mult)
     tt(ap("v0", S(64, 96)), ap("sti"), ap("jui", S(0, 32)), ALU.add)
     cp(ap("u16", 0, allc), ap("sti"))
     tt(ap("v0", S(32, 64)), ap("v0", S(0, 32)), ap("sti"), ALU.add)
     ts(ap("u16", 2, allc), ap("v0", S(64, 96)), 0.0, 4095.0, ALU.max, ALU.min)
     ts(ap("u16", 1, allc), ap("v0", S(32, 64)), SIDE[0], None, ALU.add)
-    for t in range(2):
-        fill(ap("cq%d" % t, 2, allc), (32.5, 30.5)[t])
-        fill(ap("mask%d" % t, S(4, 160, 5)), BIG)
-        fill(ap("ce%d" % t, S(1, 5 * WMAX, 5)), -K2[t])
-        fill(ap("ce%d" % t, S(2, 5 * WMAX, 5)), K2[t])
-        fill(ap("ce%d" % t, S(3, 5 * WMAX, 5)), 30.5)
-        fill(ap("ce%d" % t, S(4, 5 * WMAX, 5)), 1.0 / 64)
-    fill(ap("mask1", S(0, 160, 5)), 0.0)
-    fill(ap("mask0", S(2, 10, 5)), BIG)
-    fill(ap("mask1", S(152, 160, 5)), BIG)
-    fill(ap("floor", S(4, 5 * WMAX, 5)), BIG)
-    ts(ap("tsel"), ap("vv", S(0, 144)), r16, 15.0, ALU.add, ALU.is_equal)
-    for x in "AB":
-        fill(ap("d" + x, 1, S(0, ND)), 0.0)
 
     def exact(s, c0, c1):
         ts(ap("x16", S(3 * s, 3 * s + 3), S(c0, c1)), ap("u16", S(3 * s, 3 * s + 3), S(c0, c1)), -2048.0, None, ALU.add)
@@ -366,38 +478,32 @@ def rank_body(g, core, T, topo, rank):
 
     def rows_out(s, c0, c1):
         act(ap("fl", S(3 * s, 3 * s + 3), S(c0, c1)), ap("pq", S(0, 3), S(0, c1 - c0)), ACT.Identity,
-            bias=96.0 - 4031.0 / 16384, scale=1.0 / 128)
+            bias=97.0 - 4031.0 / 16384, scale=1.0 / 128)
 
+    ts(ap("wide", S(256, 512)), ap("base", S(384, 640)), 129.0 / 128, None, ALU.mult)
+    ts(ap("wide", S(768, 1024)), ap("base", S(384, 640)), -129.0 / 128, None, ALU.mult)
     exact(0, 0, 32)
+    fill(ap("mc", S(0, 7 * NM, NM)), BIG)
+    for nm, lo in (("sq1B", 0), ("sq1B", 64), ("sq1A", 0), ("sq1A", 64)):
+        fill(ap(nm, allw, S(lo, lo + 16)), 0.0)
+    last_sweep_matrices()
+    cp(ap("fb0", S(0, PAD)), ap("fb0", S(PAD, 2 * PAD)))
 
-    sent = 0
-    ms = split_mask(topo, core, rel[0], 4)
     rows_in(0, 0, 32)
-    rows_out(0, 0, 32)
-    first = [ap("fb0", S(0, LEAD))] + 3 * [ap("jb", S(0, 128))]
-    deps("g", first, [])
-    g.remote_dma_fused([transfer(topo, core, rel[k], ms[k], T.sem.arrj, first[k][0], first[k][0]) for k in range(4)],
-                       local_sem=T.sem.sent)
-    sent += sum(nbits(m) for m in ms)
-    for h in range(2):
-        if h == 1:
-            act(ap("fb0", S(PAD + NF, NB)), ap("fb0", S(NF, PAD + NF)), ACT.Copy)
-        deps("g", [ap("fb0", S(LEAD + 4 * h * NP, LEAD + 4 * (h + 1) * NP))], [])
-        trs = []
-        for k, c in enumerate(rel):
-            a = ap("fb0", S(LEAD + (4 * h + k) * NP, LEAD + (4 * h + k + 1) * NP))
-            trs.append(transfer(topo, core, c, ms[k], T.sem["arr%d" % h], a[0], a[0]))
-        g.remote_dma_fused(trs, local_sem=T.sem.sent)
-        sent += sum(nbits(m) for m in ms)
-    for lo in (0, 64, 32):
-        gset(ap("sq1B", allw, S(lo, lo + 16)), 16 * WMAX, 0)
+    hand([None] + 3 * [ap("jb", S(0, 128))], "arrj")
+    for j in range(2 * SUB):
+        hand([ap("fb0", part_cols(k, j)) for k in range(4)], "arr%d" % j)
+    cp(ap("fb0", S(PAD + NF, NB)), ap("fb0", S(NF, PAD + NF)))
+    for nm, lo in (("sq1B", 32), ("sq1A", 32)):
+        gset(ap(nm, allw, S(lo, lo + 16)), 16 * WMAX, 0)
+    borders(1)
 
     fs = [(rank + s) % n for s in range(n)]
     w8 = 8 * WMAX
     gset(ap("mask7"), 256, 0)
     gset(ap("floor7"), w8, -BIG)
-    for nm in ("dpf", "ce7"):
-        gset(ap(nm), w8, 0)
+    gset(ap("dpf"), w8, 0)
+    gset(ap("ce7"), 192, 0)
     gset(ap("mask7", allc, S(4, 7)), 96, -OFF)
     gset(ap("mask7", allc, 7), 32, BIG)
     gset(ap("mask7", S(30, 32), 5), 2, BIG)
@@ -405,14 +511,18 @@ def rank_body(g, core, T, topo, rank):
     for sl, val in ((0, fs[0] - fs[1]), (1, fs[1] - fs[2]), (2, fs[2] - fs[3]), (6, fs[3])):
         gset(ap("dpf", S(sl, w8, 8)), WMAX, val)
     for sl, val in ((4, -64 * K2[1]), (5, 64 * K2[1]), (6, 2048)):
-        gset(ap("ce7", S(sl, w8, 8)), WMAX, val)
+        gset(ap("ce7", S(sl, 192, 8)), 24, val)
+
+    for step in range(2, n):
+        borders(step)
 
     tiles = []
     for s in range(8):
-        tiles.append((s, "A", 0, 2 * ROWS_A[s]))
-        tiles.append((s, "B", 2 * ROWS_A[s], 32))
-    if OPT["split"]:
-        tiles[15:] = [(7, "B", 2 * ROWS_A[7], 32 - OPT["split"]), (7, "A", 32 - OPT["split"], 32)]
+        for j in range(3):
+            tiles.append((s, "AB"[len(tiles) % 2], BOUNDS[s][j], BOUNDS[s][j + 1]))
+
+    def unit(s, lower):
+        return (s, "B", BOUNDS[s][1], 32) if lower else (s, "A", 0, BOUNDS[s][1])
 
     def steps(tile, part):
         s, x, c0, c1 = tile
@@ -428,8 +538,7 @@ def rank_body(g, core, T, topo, rank):
         xt += [(o, 0, 3 * s, here), (o + 1, sh, 3 * s + 1, here), (o + 1, wr, 3 * s + 1, wrap),
                (o + 2, 0, 3 * s, vert), (o + 3, 0, 3 * s + 2, here)]
         if s < 7:
-            ft += [(0, 0, 3 * s, here), (1, sh, 3 * s, here), (1, wr, 3 * s, wrap), (2, 0, 3 * s, vert),
-                   (3, 0, 3 * s + 1, here)]
+            ft += [(0, 0, 3 * s, here), (2, 0, 3 * s, vert), (3, 0, 3 * s + 1, here)]
         calls = []
 
         def add(k, plus, minus, src, row, span):
@@ -443,7 +552,10 @@ def rank_body(g, core, T, topo, rank):
 
         if part == 0:
             for k, m, row, span in xt:
-                add(k, mat("base", m), mat("nbase", m), "x16", row, span)
+                if m and s < 7:
+                    add(k, mat("wide", m - 1), mat("wide", m + 3), "x16", row, span)
+                else:
+                    add(k, mat("base", m), mat("nbase", m), "x16", row, span)
             mm(ap("pe" + x, S(0, ns * w)), eye if s == 7 else mat("diag", 3),
                ap("ce7" if s == 7 else "ce%d" % t, S(0, ns * w)), start=True)
         else:
@@ -477,31 +589,37 @@ def rank_body(g, core, T, topo, rank):
         off = ap("u16", 3 * s + row, S(a0 + dc, a1 + dc))
         out = ap("d" + x, k, S(o + sh, o + sh + m))
         qq = ap("q", S(16 + 16 * a0 + sh, 16 + 16 * a0 + sh + m))
-        op("v", lambda e: e.tensor_tensor(out[0], win[0].indirect(off[0]), qq[0], ALU.subtract), [win, off, qq], [out])
+        op("v", lambda e: e.tensor_tensor(out[0], win[0].indirect(off[0]), qq[0], ALU.subtract), [win, off, qq], [out],
+           CALL + LOOKUP * m * CYCLE)
         act(ap("sq%d%s" % (t, x), S(a0 - c0, a1 - c0), S(16 * k, 16 * k + 16)), ap("d" + x, k, S(o, o + m)), ACT.Square)
 
-    def side_cols(tile):
-        return min(OPT["side"][tile[0] % 2], tile[3] - tile[2])
+    def side_parts(tile):
+        t, w = tile[0] % 2, tile[3] - tile[2]
+        return [(3, min(OPT["side"][t], w)), (2 * t, min(OPT["more"][t], w))]
 
-    def side_gather(tile):
+    def side_bank(tile, m):
+        return ap("p7B", S(0, m // 8), S(0, 8)) if tile[1] == "B" and tile[0] < 6 else ap("pg", S(0, m))
+
+    def side_gather(tile, j):
         s, x, c0, c1 = tile
-        u = side_cols(tile)
-        win = ap("fb%d" % (s // 2), S(PAD, PAD + NF))
-        off = ap("u16", 3 * s + 2, S(c0, c0 + u))
-        out = ap("gs", S(0, 16 * u))
+        k, u = side_parts(tile)[j]
+        base, row, dc = (0, 0, 2) if k == 2 else (PAD, 2 if k else 0, 0)
+        win = ap("fb%d" % (s // 2), S(base, base + NF))
+        off = ap("u16", 3 * s + row, S(c0 + dc, c0 + dc + u))
+        out = ap("gs", "AB".index(x), S(0, 16 * u))
         op("a", lambda e: e.activation(out[0], win[0].indirect(off[0]), ACT.Identity, bias=0.0, scale=-1.0),
-           [win, off], [out])
+           [win, off], [out], CALL + LOOKUP * 16 * u * CYCLE)
 
-    def side_diff(tile):
+    def side_diff(tile, j):
         s, x, c0, c1 = tile
-        m = 16 * side_cols(tile)
-        mm(ap("pg", S(0, m)), eye, ap("q", S(16 + 16 * c0, 16 + 16 * c0 + m)), start=True)
-        mm(ap("pg", S(0, m)), eye, ap("gs", S(0, m)), stop=True)
+        m = 16 * side_parts(tile)[j][1]
+        mm(side_bank(tile, m), eye, ap("q", S(16 + 16 * c0, 16 + 16 * c0 + m)), start=True)
+        mm(side_bank(tile, m), eye, ap("gs", "AB".index(x), S(0, m)), stop=True)
 
-    def side_square(tile):
+    def side_square(tile, j):
         s, x, c0, c1 = tile
-        u = side_cols(tile)
-        act(ap("sq%d%s" % (s % 2, x), S(0, u), S(48, 64)), ap("pg", S(0, 16 * u)), ACT.Square)
+        k, u = side_parts(tile)[j]
+        act(ap("sq%d%s" % (s % 2, x), S(0, u), S(16 * k, 16 * k + 16)), side_bank(tile, 16 * u), ACT.Square)
 
     def least(s, c0, c1):
         return ap("mc", S(NM * s + 5 * c0 + 4, NM * s + 5 * c1, 5))
@@ -546,7 +664,8 @@ def rank_body(g, core, T, topo, rank):
                 act(ap("oc", S(c0, c1)), ap(mb, S(mo + 7, mo + m, 8)), ACT.Identity, bias=OFF)
 
         def three():
-            scan(z, ni, ap("pe" + x, S(0, m)), 0.0, ALU.mult, ALU.add)
+            u = unit(s, c0 > 0)
+            scan(z, ni, ap("pe" + u[1], S(ns * (c0 - u[2]), ns * (c1 - u[2]))), 0.0, ALU.mult, ALU.add)
             if s == 7:
                 scan(ap("zf" + x, S(0, m)), ni, ap("dpf", S(0, m)), 0.0, ALU.mult, ALU.add)
 
@@ -556,70 +675,56 @@ def rank_body(g, core, T, topo, rank):
                 cp(ap("of", S(c0, c1)), ap("zf" + x, S(6, m, 8)))
                 return
             v, r = ap("z" + x, S(3, m, 5)), 3 * (s + 1)
-            ts(ap("u16", r, S(c0, c1)), v, SHRINK, 0.75 * SHRINK + 0.25, ALU.mult, ALU.add)
+            ts(ap("u16", r, S(c0, c1)), v, SHRINK, 0.25 - 0.25 * SHRINK, ALU.mult, ALU.add)
             ts(ap("u16", r + 2, S(c0, c1)), ap("z" + x, S(4, m, 5)), SHRINK, 4095.0, ALU.mult, ALU.min)
-            ts(ap("u16", r + 1, S(c0, c1)), v, SHRINK, 0.75 * SHRINK + SIDE[(s + 1) % 2], ALU.mult, ALU.add)
+            ts(ap("u16", r + 1, S(c0, c1)), v, SHRINK, SIDE[(s + 1) % 2] - 0.25 * SHRINK, ALU.mult, ALU.add)
 
         return [one, two, three, four]
 
-    nt = len(tiles)
-    for i in range(nt + 1):
-        tile = tiles[i] if i < nt else None
-        prev = tiles[i - 1] if i >= 1 else None
-        made = tiles[i - 2] if 2 <= i < 16 else None
-        todo = pick(prev) if prev else []
-        if tile:
-            t, u = tile[0] % 2, side_cols(tile)
-            w = tile[3] - tile[2]
-            order = [(2, 0, w), (1, 0, w)] + ([(0, 0, w)] if t == 0 else []) + ([(3, u, w)] if u < w else [])
-            if i == 0:
-                order.append(order.pop(0))
-            cut = order[-1][2] - OPT["cut"][t]
-            if OPT["cut"][t] and cut > order[-1][1]:
-                order[-1:] = [(order[-1][0], order[-1][1], cut), (order[-1][0], cut, w)]
-            if i == nt - 4:
-                aset(ap("mask7", S(1, 32, 2), 4), 16, big15)
-            for c in OPT["last"] if i == nt - 1 else OPT["plan"][t]:
-                if c == "g" and order:
-                    gather(tile, *order.pop(0))
-                if c == "G":
-                    while order:
-                        gather(tile, *order.pop(0))
-                if c == "p" and todo:
-                    todo.pop(0)()
-                if c == "a" and u:
-                    side_gather(tile)
-                if c == "d" and u:
-                    side_diff(tile)
-                if c == "q" and u:
-                    side_square(tile)
-                if c == "s" and prev:
-                    sums(prev)
-                if c == "f" and prev:
-                    steps(prev, 1)
-                    jumps(prev)
-                if c == "x" and made:
-                    exact(tile[0], made[2], made[3])
-                if c == "r" and made:
-                    rows_in(tile[0], made[2], made[3])
-                if c == "o" and made:
-                    rows_out(tile[0], made[2], made[3])
-                if c == "m":
-                    sums_pre(tile)
-                if c == "e":
-                    steps(tile, 0)
-        else:
-            steps(prev, 1)
-            sums(prev)
-        for f in todo:
-            f()
+    nt, per = len(tiles), 3
+    for i, tile in enumerate(tiles):
+        s, w, j = tile[0], tile[3] - tile[2], i % per
+        if i >= per and j in (0, per - 1):
+            made = unit(s - 1, j > 0)
+            place[0] = i + (OPT["x"][2 * (s % 2) + (j > 0)] if i < nt - 1 else OPT["end"][3])
+            task(exact, s, made[2], made[3])
+            task(rows_in, s, made[2], made[3])
+            task(rows_out, s, made[2], made[3])
+        if i == 0:
+            task(rows_out, 0, 0, 32)
+        if i == 0:
+            place[0] = 1.95
+            task(second_sweep_constants)
+        if i == nt - 2 * per:
+            task(act, ap("mask7", S(1, 32, 2), 4), ap("fl", 15, S(0, 16)), ACT.Identity, big15, 0.0)
+        aside = dict(side_parts(tile))
+        for k, part in enumerate(side_parts(tile)):
+            if part[1]:
+                task(side_gather, tile, k)
+                task(side_diff, tile, k)
+                task(side_square, tile, k)
+        for turn, k in enumerate(OPT["order"][s % 2] if i % (2 * per) else (1, 0, 2, 3)):
+            place[0] = i + (OPT["g"][turn] if i < nt - 1 else OPT["end"][turn])
+            if aside.get(k, 0) < w:
+                task(gather, tile, k, aside.get(k, 0), w)
+        task(sums_pre, tile)
+        task(sums, tile)
+        if j == 0 or j == per - 1:
+            task(steps, unit(s, j > 0), 0)
+            task(steps, unit(s, j > 0), 1)
+            task(jumps, unit(s, j > 0))
+        for late in ([tile] if j == 0 else tiles[i - 1:i + 1] if j == per - 1 else []):
+            for turn, f in enumerate(pick(late)):
+                place[0] = min(tiles.index(late) + per - 1, nt + OPT["end"][4]) + OPT["p"][turn]
+                task(f)
+    flush()
 
     outs = []
     a = ap("oc"); outs.append(dma("s", T.yc[:], a[0], "out0", [a], []))
     a = ap("op"); outs.append(dma("a", T.yp[:], a[0], "out1", [a], []))
     a = ap("of"); outs.append(dma("s", T.yf[:], a[0], "out2", [a], []))
     waits = [("fj%d" % k, nbits(topo.mask(relays_of(T, topo, T.cores[(rank + k) % n])[k], core)), {}) for k in range(1, n)]
-    finish("g", [("sent", sent, {})] + waits + outs)
+    finish("g", [("sent", sent[0], {})] + waits + outs)
 
 
 def rank_program(g, core, T, topo):

import numpy as np
from concourse.bass import DstId, RemoteDMATransfer
from concourse.mybir import AluOpType, ActivationFunctionType

NF = 4096
PAD = 64
NB = NF + 2 * PAD
LEAD = 128
NP = (NF - 4 * LEAD) // 8
SUB = 2
BIG = 8192.0
OFF = 2048.0
OPT = {
    "rows0": (8, 13),
    "g": (0.1, 0.3, 0.5, 0.7),
    "p": (0.0, 0.2, 0.4, 0.9),
    "x": (0.6, 0.15, 0.6, 0.15),
    "end": (0.1, 0.3, 0.5, 0.15, 1.0),
    "side": [20, 6],
    "last": "asgxrdfomegqG",
    "first": "aAsgdfgqDmeGQc",
    "plan": ["aAsdfgqDgxprgmGpQppeo", "sagdqgpfgxrpoeGpmp"],
    "cut": [0, 0],
    "more": [0, 0],
    "order": [(2, 1, 0, 3), (2, 1, 3)],
    "split": 0,
}
BOUNDS = [[0] + [2 * (r - (s + 1) // 2) for r in OPT["rows0"]] + [32] for s in range(8)]
WMAX = max(b[j + 1] - b[j] for b in BOUNDS for j in range(3))
CYCLE, CALL, WAKE, LOOKUP, SLACK = 0.00083, 0.05, 0.2, 1.56, 0.03
ND = 16 * WMAX + 32
NM = 164

SCRATCH = {
    "jb": ("sbuf", [128, 512], "bfloat16"),
    "q": ("sbuf", [128, 544], "bfloat16"),
    "gs": ("sbuf", [128, 2, 16 * WMAX], "bfloat16"),
    "sti": ("sbuf", [128, 32], "int32"),
    "jui": ("sbuf", [128, 64], "int32"),
    "jt": ("sbuf", [128, 128], "int32"),
    "xi": ("sbuf", [128, 32], "int32"),
    "v0": ("sbuf", [128, 96], "float32"),
    "vv": ("sbuf", [128, 144], "bfloat16"),
    "pi": ("sbuf", [128, 8], "int32"),
    "col": ("sbuf", [128, 8], "float32"),
    "tsel": ("sbuf", [128, 144], "bfloat16"),
    "base": ("sbuf", [128, 640], "bfloat16"),
    "nbase": ("sbuf", [128, 640], "bfloat16"),
    "wide": ("sbuf", [128, 1024], "bfloat16"),
    "diag": ("sbuf", [128, 896], "bfloat16"),
    "mask0": ("sbuf", [128, 160], "bfloat16"),
    "mask1": ("sbuf", [128, 160], "bfloat16"),
    "mask7": ("sbuf", [128, 32, 8], "bfloat16"),
    "ce0": ("sbuf", [128, 120], "float16"),
    "ce1": ("sbuf", [128, 120], "float16"),
    "ce7": ("sbuf", [128, 192], "bfloat16"),
    "cq0": ("sbuf", [128, 3, 32], "bfloat16"),
    "cq1": ("sbuf", [128, 3, 32], "bfloat16"),
    "floor": ("sbuf", [128, 5 * WMAX], "float32"),
    "floor7": ("sbuf", [128, 8 * WMAX], "float32"),
    "dpf": ("sbuf", [128, 8 * WMAX], "float32"),
    "u16": ("sbuf", [128, 24, 32], "uint16"),
    "x16": ("sbuf", [128, 24, 32], "float16"),
    "fl": ("sbuf", [128, 24, 32], "bfloat16"),
    "mc": ("sbuf", [128, 7 * NM], "float16"),
    "m7": ("sbuf", [128, 260], "float32"),
    "oc": ("sbuf", [128, 32], "float32"),
    "of": ("sbuf", [128, 32], "float32"),
    "op": ("sbuf", [128, 32], "float32"),
    "pq": ("psum", [128, 16, 32], "float32"),
    "pg": ("psum", [128, 512], "float32"),
}
for _k in range(4):
    SCRATCH["fb%d" % _k] = ("sbuf", [128, NB], "bfloat16")
for _x in "AB":
    SCRATCH["d" + _x] = ("sbuf", [128, 4, ND], "bfloat16")
    SCRATCH["sq0" + _x] = ("sbuf", [128, WMAX, 80], "bfloat16")
    SCRATCH["sq1" + _x] = ("sbuf", [128, WMAX, 80], "bfloat16")
    SCRATCH["ni" + _x] = ("sbuf", [128, 8 * WMAX], "bfloat16")
    SCRATCH["z" + _x] = ("sbuf", [128, 8 * WMAX], "float32")
    SCRATCH["zf" + _x] = ("sbuf", [128, 8 * WMAX], "float32")
    SCRATCH["ps" + _x] = ("psum", [128, 512], "float32")
    SCRATCH["pe" + _x] = ("psum", [128, 512], "float32")
    SCRATCH["p7" + _x] = ("psum", [128, 64, 8], "float32")

SEMAPHORES = ["sv", "sa", "sp", "sq", "ld0", "ld1", "lp", "lj", "ls", "lq", "sent", "arrl", "arrj", "arr0", "arr1", "arr2", "arr3",
              "fj1", "fj2", "fj3", "fa1", "fa2", "fa3", "out0", "out1", "out2"]


def relays_of(T, topo, src):
    others = [d for d in T.cores if d != src]
    rel = [c for c in topo.cores_of(src) if c != src and all(topo.may_write(c, d) for d in others)]
    far = [c for c in rel if topo.die(c) != topo.die(src)]
    near = [c for c in rel if topo.die(c) == topo.die(src)]
    out = []
    while far or near:
        if far:
            out.append(far.pop(0))
        if near:
            out.append(near.pop(0))
    return out[:4]


def nbits(m):
    return bin(m).count("1")


def split_mask(topo, src, dst, parts):
    e = topo.engines(src, dst)
    k = len(e) // parts
    return [sum(1 << x for x in e[i * k:(i + 1) * k]) for i in range(parts)]


def transfer(topo, src, dst, mask, sem, a, b):
    rid, pid = topo.addr(dst, src)
    return RemoteDMATransfer(dst_ids=[DstId(rid=rid, pnc=pid)], dma_engine_mask=mask, remote_sem=sem, src=a, dst=b)


def lead_cols(k):
    return slice(PAD + k * LEAD, PAD + (k + 1) * LEAD)


def piece_cols(k, h):
    lo = PAD + 4 * LEAD + (4 * h + k) * NP
    return slice(lo, lo + NP)


def part_cols(k, j):
    lo = piece_cols(k, j // SUB).start + (j % SUB) * NP // SUB
    return slice(lo, lo + NP // SUB)


def relay_program(g, core, T, topo, src, k):
    n = len(T.cores)
    r = T.rank_of(src)
    got = nbits(split_mask(topo, src, core, 4)[k])
    total = [0]

    def send(step, name, dst, a, sem):
        d = T.cores[(r - step) % n]
        rid, pid = topo.addr(d, core)
        m = topo.mask(core, d)
        g.remote_dma(T[name][:, dst], a, T.sem[sem], T.sem.sent, pid, rid, m)
        total[0] += nbits(m)

    g.wait_ge(T.sem.arrl, got)
    send(1, "fb1", lead_cols(k), T.fb0[:, lead_cols(k)], "fa1")
    if k >= 1:
        g.wait_ge(T.sem.arrj, got)
        send(k, "jb", slice(128 * k, 128 * k + 128), T.jb[:, 0:128], "fj%d" % k)
    for j in range(2 * SUB):
        g.wait_ge(T.sem["arr%d" % j], got)
        send(1, "fb1", part_cols(k, j), T.fb0[:, part_cols(k, j)], "fa1")
    for step in range(2, n):
        d = T.cores[(r - step) % n]
        ms = split_mask(topo, core, d, 2)
        send(step, "fb%d" % step, lead_cols(k), T.fb0[:, lead_cols(k)], "fa%d" % step)
        g.remote_dma_fused([transfer(topo, core, d, ms[h], T.sem["fa%d" % step], T.fb0[:, piece_cols(k, h)],
                                     T["fb%d" % step][:, piece_cols(k, h)]) for h in range(2)], local_sem=T.sem.sent)
        total[0] += sum(nbits(m) for m in ms)
    g.wait_ge(T.sem.sent, total[0])


def make_emitter(g, T):
    queues = {"v": g.vector, "a": g.scalar, "p": g.tensor, "g": g, "s": g.sync}
    own = {"v": "sv", "a": "sa", "p": "sp", "g": "sq"}
    count = {"sv": 0, "sa": 0, "sp": 0, "sq": 0}
    known = {q: {} for q in queues}
    hist = {}
    grids = {}
    held = []
    place = [0.0]

    def ap(name, *idx):
        if name not in grids:
            shp = SCRATCH[name][1][1:]
            grids[name] = np.arange(int(np.prod(shp))).reshape(shp)
        full = (slice(None),) + tuple(idx)
        if SCRATCH[name][0] == "psum":
            bits = 1
        else:
            flags = np.zeros(grids[name].size, np.uint8)
            flags[grids[name][tuple(idx)].reshape(-1) if idx else slice(None)] = 1
            bits = int.from_bytes(np.packbits(flags, bitorder="little").tobytes(), "little")
        return (T[name][full], name, bits, int(grids[name][tuple(idx)].size if idx else grids[name].size))

    def wait(q, ev):
        sem, val, clock = ev
        if known[q].get(sem, 0) >= val:
            return
        queues[q].wait_ge(T.sem[sem], val)
        known[q][sem] = val
        for s, v in clock.items():
            if known[q].get(s, 0) < v:
                known[q][s] = v

    def note(q, ev, reads, writes):
        for a in writes:
            h = hist.setdefault(a[1], [])
            h[:] = [e for e in h if e[1] & ~a[2]]
            h.append((ev, a[2], True, q))
        for a in reads:
            hist.setdefault(a[1], []).append((ev, a[2], False, q))

    def deps(q, reads, writes):
        need = []
        for a in reads:
            psum = SCRATCH[a[1]][0] == "psum"
            for e in hist.get(a[1], []):
                if e[1] & a[2] and (e[2] or (psum and e[3] != q)):
                    need.append(e[0])
        for a in writes:
            psum = SCRATCH[a[1]][0] == "psum"
            for e in hist.get(a[1], []):
                if e[1] & a[2] and not (psum and q == "p" and e[3] == "p"):
                    need.append(e[0])
        best = {}
        for ev in need:
            if ev[0] not in best or best[ev[0]][1] < ev[1]:
                best[ev[0]] = ev
        for ev in best.values():
            wait(q, ev)

    def op(q, fn, reads, writes, cost=0.0):
        if held:
            if q == "p":
                held[-1].append((q, fn, reads, writes, cost))
            else:
                held.extend([[(q, fn, reads, writes, cost, (place[0], len(held)))], []])
            return None
        deps(q, reads, writes)
        sem = own[q]
        count[sem] += 1
        fn(queues[q]).then_inc(T.sem[sem], 1)
        ev = (sem, count[sem], dict(known[q]))
        note(q, ev, reads, writes)
        return ev

    def dma(q, out, in_, sem, reads, writes):
        deps(q, reads, writes)
        queues[q].dma_start(out, in_).then_inc(T.sem[sem], 16)
        ev = (sem, 16, dict(known[q]))
        note("dma", ev, reads, writes)
        return ev

    def landed(a, sem, val):
        note("dma", (sem, val, {}), [], [a])

    def finish(q, evs):
        for sem, v in count.items():
            if v:
                wait(q, (sem, v, {}))
        for ev in evs:
            wait(q, ev)

    def task(fn, *args):
        held.append([])
        fn(*args)

    def flush():
        tasks = [t for t in held if t]
        del held[:]
        seen, before, after = {}, [], [[] for t in tasks]
        for i, t in enumerate(tasks):
            need = set()
            for c in t:
                for a, wr in [(a, False) for a in c[2]] + [(a, True) for a in c[3]]:
                    wr = wr or SCRATCH[a[1]][0] == "psum"
                    need.update(j for j, bits, w in seen.get(a[1], []) if bits & a[2] and (w or wr) and j != i)
            for c in t:
                for a in c[3]:
                    seen[a[1]] = [e for e in seen.get(a[1], []) if e[1] & ~a[2]] + [(i, a[2], True)]
                for a in c[2]:
                    seen.setdefault(a[1], []).append((i, a[2], SCRATCH[a[1]][0] == "psum"))
            before.append(need)
            for j in need:
                after[j].append(i)
        row = sorted((i for i, t in enumerate(tasks) if t[0][0] == "v"), key=lambda i: tasks[i][0][5])
        free_of = set()
        for j, i in zip(row, row[1:]):
            if j not in before[i]:
                before[i].add(j)
                after[j].append(i)
                free_of.add((j, i))
        span = [sum(c[4] for c in t) for t in tasks]
        lag = lambda j, i: 0.0 if tasks[j][0][0] == tasks[i][0][0] == "p" or (j, i) in free_of else WAKE
        way = list(span)
        chain, cnt = [i for i in range(len(tasks)) if not before[i]], [len(b) for b in before]
        for i in chain:
            for j in after[i]:
                cnt[j] -= 1
                if not cnt[j]:
                    chain.append(j)
        for i in reversed(chain):
            way[i] += max([lag(i, j) + way[j] for j in after[i]], default=0.0)
        left, end, free = [len(b) for b in before], {}, {q: 0.0 for q in queues}
        ready = [i for i in range(len(tasks)) if not left[i]]
        while ready:
            start = {i: max([free[tasks[i][0][0]]] + [end[j] + lag(j, i) for j in before[i]]) for i in ready}
            soon = min(start.values())
            i = max((i for i in ready if start[i] <= soon + SLACK), key=lambda i: way[i])
            ready.remove(i)
            end[i] = free[tasks[i][0][0]] = start[i] + span[i]
            for c in tasks[i]:
                op(*c[:4])
            for j in after[i]:
                left[j] -= 1
                if not left[j]:
                    ready.append(j)

    return ap, op, dma, landed, deps, finish, task, flush, place


def rank_body(g, core, T, topo, rank):
    n = len(T.cores)
    ALU, ACT = AluOpType, ActivationFunctionType
    ap, op, dma, landed, deps, finish, task, flush, place = make_emitter(g, T)
    S = slice

    def small(out):
        return max(64, out[3]) * CYCLE

    def ts(out, in0, s1, s2, o0, o1=None):
        a1 = s1[0] if isinstance(s1, tuple) else s1
        a2 = s2[0] if isinstance(s2, tuple) else s2
        rd = [in0] + [s for s in (s1, s2) if isinstance(s, tuple)]
        if o1 is None:
            return op("v", lambda e: e.tensor_scalar(out[0], in0[0], a1, None, o0), rd, [out], small(out))
        return op("v", lambda e: e.tensor_scalar(out[0], in0[0], a1, a2, o0, o1), rd, [out], small(out))

    def tt(out, in0, in1, o):
        return op("v", lambda e: e.tensor_tensor(out[0], in0[0], in1[0], o), [in0, in1], [out], small(out))

    def cp(out, in0):
        return op("v", lambda e: e.tensor_copy(out[0], in0[0]), [in0], [out], small(out))

    def fill(out, val):
        return op("v", lambda e: e.memset(out[0], val), [], [out], small(out))

    def scan(out, d0, d1, init, o0, o1):
        return op("v", lambda e: e.tensor_tensor_scan(out[0], d0[0], d1[0], init, o0, o1), [d0, d1], [out], small(out))

    def act(out, in0, func, bias=0.0, scale=1.0):
        b = bias[0] if isinstance(bias, tuple) else bias
        rd = [in0] + ([bias] if isinstance(bias, tuple) else [])
        return op("a", lambda e: e.activation(out[0], in0[0], func, bias=b, scale=scale), rd, [out], CALL + small(out))

    def mm(out, lhs, rhs, start=False, stop=False):
        return op("p", lambda e: e.matmul(out[0], lhs[0], rhs[0], start, stop), [lhs, rhs], [out], small(out) / 2)

    def aset(out, cnt, val):
        act(out, ap("vv", S(0, cnt)), ACT.Identity, bias=val, scale=0.0)

    def gset(out, cnt, val):
        op("g", lambda e: e.iota(out[0], [[0, cnt]], int(val), 0, allow_small_or_imprecise_dtypes=True), [], [out])

    allc, allw = S(0, 32), S(0, WMAX)
    rel = relays_of(T, topo, core)

    sent = [0]

    def hand(parts, sem):
        ms = split_mask(topo, core, rel[0], 4)
        ks = [k for k in range(4) if parts[k]]
        deps("g", [parts[k] for k in ks], [])
        g.remote_dma_fused([transfer(topo, core, rel[k], ms[k], T.sem[sem], parts[k][0], parts[k][0]) for k in ks],
                           local_sem=T.sem.sent)
        sent[0] += sum(nbits(ms[k]) for k in ks)

    def borders(step):
        for e0, r0 in ((PAD + NF, NF), (0, PAD)):
            edge, row = ap("fb%d" % step, S(e0, e0 + PAD)), ap("fb%d" % step, S(r0, r0 + PAD))
            op("g", lambda e: e.affine_select(edge[0], row[0], [[0, PAD]], ALU.is_ge, 0.0, 0, 0), [row], [edge])

    a = ap("fb0", S(PAD, PAD + 4 * LEAD)); dma("s", a[0], T.fr[:, 0:4 * LEAD], "lp", [], [a])
    a = ap("jui"); dma("a", a[0], T.ju[:], "lj", [], [a])
    a = ap("sti"); dma("a", a[0], T.st[:], "ls", [], [a])
    a = ap("q", S(16, 528)); dma("a", a[0], T.qu[:], "lq", [], [a])
    for h in range(2):
        lo, hi = piece_cols(0, h).start, piece_cols(3, h).stop
        a = ap("fb0", S(lo, hi)); dma("s", a[0], T.fr[:, lo - PAD:hi - PAD], "ld%d" % h, [], [a])
    for step in range(1, n):
        far = relays_of(T, topo, T.cores[(rank + step) % n])
        landed(ap("jb", S(128 * step, 128 * step + 128)), "fj%d" % step, nbits(topo.mask(far[step], core)))
        landed(ap("fb%d" % step, S(PAD, PAD + NF)), "fa%d" % step,
               (1 + 2 * SUB if step == 1 else 2) * sum(nbits(topo.mask(c, core)) for c in far))

    a2 = ap("pi", S(0, 1))
    op("g", lambda e: e.iota(a2[0], [[1, 1]], 0, 1), [], [a2])
    a3 = ap("vv")
    op("g", lambda e: e.iota(a3[0], [[1, 144]], 0, -1, allow_small_or_imprecise_dtypes=True), [], [a3])

    K2 = (195.0, 193.0)
    w5 = 5 * WMAX
    fill(ap("mask0"), -OFF)
    fill(ap("ce0"), 0.0)
    fill(ap("cq0"), 0.0)
    fill(ap("floor"), -BIG)
    ts(ap("pi", S(4, 5)), ap("pi", S(0, 1)), 15, None, ALU.bitwise_and)
    fill(ap("sq0A", allw, S(64, 80)), 0.0)
    r16 = ap("col", S(0, 1))
    cp(r16, ap("pi", S(4, 5)))
    fill(ap("sq0B", allw, S(64, 80)), 0.0)
    for a, cnt, val in ((ap("q", S(0, 16)), 16, 0), (ap("q", S(528, 544)), 16, 0), (ap("sq0B", S(0, 2), S(32, 48)), 32, 0),
                        (ap("mask0", S(2, 10, 5)), 2, BIG), (ap("floor", S(4, w5, 5)), WMAX, BIG)):
        gset(a, cnt, val)
    hand([ap("fb0", lead_cols(k)) for k in range(4)], "arrl")
    for a, cnt, val in ((ap("sq0A", S(0, 2), S(32, 48)), 32, 0.0), (ap("cq0", 2, allc), 32, 32.5),
                        (ap("dA", 1, S(16, 17)), 1, 0.0), (ap("dB", 1, S(16, 17)), 1, 0.0),
                        (ap("dB", 1, S(176, ND)), ND - 176, 0.0), (ap("mask0", S(4, 160, 5)), 32, BIG)):
        aset(a, cnt, val)
    ne15, ne0, eq15, eq0, big15, big0 = [ap("col", S(i, i + 1)) for i in range(1, 7)]
    ts(ne15, r16, 15.0, None, ALU.not_equal)
    ts(eq15, r16, 15.0, None, ALU.is_equal)
    ts(big0, r16, 0.0, BIG, ALU.is_equal, ALU.mult)
    ts(ne0, r16, 0.0, None, ALU.not_equal)
    ts(eq0, r16, 0.0, None, ALU.is_equal)
    ts(big15, r16, 15.0, BIG, ALU.is_equal, ALU.mult)
    ts(ap("col", S(5, 7)), ap("col", S(5, 7)), -OFF, None, ALU.add)

    v128 = ap("vv", S(0, 128))
    for i, (k, c) in enumerate([(0.0, 1.0), (1.0, ne15), (-15.0, eq15), (-1.0, ne0), (15.0, eq0)]):
        ts(ap("base", S(128 * i, 128 * i + 128)), v128, k, c, ALU.is_equal, ALU.mult)

    def mat(name, i):
        return ap(name, S(128 * i, 128 * i + 128))

    eye = mat("base", 0)
    act(mat("nbase", 0), eye, ACT.Identity, scale=-1.0)
    for i, val in enumerate((1.0 / 64, 129.0, -129.0, 64.5, 129.0 / 128)):
        act(mat("diag", i), eye, ACT.Identity, scale=val)

    def last_sweep_matrices():
        act(ap("nbase", S(384, 640)), ap("base", S(384, 640)), ACT.Identity, scale=-1.0)
        act(mat("diag", 5), eye, ACT.Identity, scale=128.0)
        act(mat("diag", 6), eye, ACT.Identity, scale=-128.0)

    aset(ap("mask0", S(1, 160, 10)), 16, big0)
    ts(ap("tsel"), ap("vv", S(0, 144)), r16, 15.0, ALU.add, ALU.is_equal)
    for sl, val in enumerate((-1.5, 1.5 - K2[0], K2[0], 30.5)):
        fill(ap("ce0", S(sl, 120, 5)), val)
    act(ap("wide", S(0, 256)), ap("base", S(128, 384)), ACT.Identity, scale=129.0 / 128)
    act(ap("wide", S(512, 768)), ap("base", S(128, 384)), ACT.Identity, scale=-129.0 / 128)

    def second_sweep_constants():
        fill(ap("mask1"), -OFF)
        cp(ap("ce1"), ap("ce0"))
        fill(ap("cq1"), 0.0)
        fill(ap("m7", S(0, 1)), BIG)
        fill(ap("mask1", S(4, 160, 5)), BIG)
        fill(ap("ce1", S(1, 120, 5)), 1.5 - K2[1])
        fill(ap("ce1", S(2, 120, 5)), K2[1])
        fill(ap("cq1", 2, allc), 30.5)
        fill(ap("mask1", S(0, 160, 5)), 0.0)
        fill(ap("mask1", S(152, 160, 5)), BIG)
        ts(ap("mask1", S(6, 160, 10)), ap("vv", S(0, 16)), 0.0, big15, ALU.mult, ALU.add)

    SHRINK, SIDE = 128.0 / 129, (0.5 + 62.5 / 129, 0.5 / 129 - 0.5)
    ts(ap("jt", S(0, 64)), ap("jui"), 6, None, ALU.arith_shift_right)
    ts(ap("jt", S(64, 128)), ap("jui"), 63, None, ALU.bitwise_and)
    ts(ap("xi"), ap("sti"), 63, None, ALU.bitwise_and)
    cp(ap("jb", S(0, 128)), ap("jt"))
    ts(ap("v0", S(0, 32)), ap("xi"), -1.0 / 129, None, ALU.mult)
    tt(ap("v0", S(64, 96)), ap("sti"), ap("jui", S(0, 32)), ALU.add)
    cp(ap("u16", 0, allc), ap("sti"))
    tt(ap("v0", S(32, 64)), ap("v0", S(0, 32)), ap("sti"), ALU.add)
    ts(ap("u16", 2, allc), ap("v0", S(64, 96)), 0.0, 4095.0, ALU.max, ALU.min)
    ts(ap("u16", 1, allc), ap("v0", S(32, 64)), SIDE[0], None, ALU.add)

    def exact(s, c0, c1):
        ts(ap("x16", S(3 * s, 3 * s + 3), S(c0, c1)), ap("u16", S(3 * s, 3 * s + 3), S(c0, c1)), -2048.0, None, ALU.add)

    def rows_in(s, c0, c1):
        w = c1 - c0
        mm(ap("pq", S(0, 3), S(0, w)), eye, ap("cq%d" % (s % 2), S(0, 3), S(0, w)), start=True)
        mm(ap("pq", S(0, 2), S(0, w)), eye, ap("x16", S(3 * s, 3 * s + 3, 2), S(c0, c1)))
        mm(ap("pq", 2, S(0, w)), mat("diag", 0), ap("x16", 3 * s, S(c0, c1)), stop=True)

    def rows_out(s, c0, c1):
        act(ap("fl", S(3 * s, 3 * s + 3), S(c0, c1)), ap("pq", S(0, 3), S(0, c1 - c0)), ACT.Identity,
            bias=97.0 - 4031.0 / 16384, scale=1.0 / 128)

    ts(ap("wide", S(256, 512)), ap("base", S(384, 640)), 129.0 / 128, None, ALU.mult)
    ts(ap("wide", S(768, 1024)), ap("base", S(384, 640)), -129.0 / 128, None, ALU.mult)
    exact(0, 0, 32)
    fill(ap("mc", S(0, 7 * NM, NM)), BIG)
    for nm, lo in (("sq1B", 0), ("sq1B", 64), ("sq1A", 0), ("sq1A", 64)):
        fill(ap(nm, allw, S(lo, lo + 16)), 0.0)
    last_sweep_matrices()
    cp(ap("fb0", S(0, PAD)), ap("fb0", S(PAD, 2 * PAD)))

    rows_in(0, 0, 32)
    hand([None] + 3 * [ap("jb", S(0, 128))], "arrj")
    for j in range(2 * SUB):
        hand([ap("fb0", part_cols(k, j)) for k in range(4)], "arr%d" % j)
    cp(ap("fb0", S(PAD + NF, NB)), ap("fb0", S(NF, PAD + NF)))
    for nm, lo in (("sq1B", 32), ("sq1A", 32)):
        gset(ap(nm, allw, S(lo, lo + 16)), 16 * WMAX, 0)
    borders(1)

    fs = [(rank + s) % n for s in range(n)]
    w8 = 8 * WMAX
    gset(ap("mask7"), 256, 0)
    gset(ap("floor7"), w8, -BIG)
    gset(ap("dpf"), w8, 0)
    gset(ap("ce7"), 192, 0)
    gset(ap("mask7", allc, S(4, 7)), 96, -OFF)
    gset(ap("mask7", allc, 7), 32, BIG)
    gset(ap("mask7", S(30, 32), 5), 2, BIG)
    gset(ap("floor7", S(7, w8, 8)), WMAX, BIG)
    for sl, val in ((0, fs[0] - fs[1]), (1, fs[1] - fs[2]), (2, fs[2] - fs[3]), (6, fs[3])):
        gset(ap("dpf", S(sl, w8, 8)), WMAX, val)
    for sl, val in ((4, -64 * K2[1]), (5, 64 * K2[1]), (6, 2048)):
        gset(ap("ce7", S(sl, 192, 8)), 24, val)

    for step in range(2, n):
        borders(step)

    tiles = []
    for s in range(8):
        for j in range(3):
            tiles.append((s, "AB"[len(tiles) % 2], BOUNDS[s][j], BOUNDS[s][j + 1]))

    def unit(s, lower):
        return (s, "B", BOUNDS[s][1], 32) if lower else (s, "A", 0, BOUNDS[s][1])

    def steps(tile, part):
        s, x, c0, c1 = tile
        w, t = c1 - c0, s % 2
        ns, o = (8, 3) if s == 7 else (5, 0)
        sh, wr, dc = (1, 2, -2) if t == 0 else (3, 4, 2)
        b0, b1 = max(c0, -dc), min(c1, 32 - dc)
        here, vert = (c0, c1, 1, 0), (b0, b1, 1, dc)
        wrap = (c0 + 1, c1, 2, -1) if t == 0 else (c0, c1, 2, 1)
        xt, ft = [], []
        if s == 7:
            xt += [(j, 0, 3 * (2 * j + 2), here) for j in range(3)]
        xt += [(o, 0, 3 * s, here), (o + 1, sh, 3 * s + 1, here), (o + 1, wr, 3 * s + 1, wrap),
               (o + 2, 0, 3 * s, vert), (o + 3, 0, 3 * s + 2, here)]
        if s < 7:
            ft += [(0, 0, 3 * s, here), (2, 0, 3 * s, vert), (3, 0, 3 * s + 1, here)]
        calls = []

        def add(k, plus, minus, src, row, span):
            a0, a1, st, d = span
            rhs = ap(src, row, S(a0 + d, a1 + d if st == 1 else a1, st))
            cnt = len(range(a0, a1, st))
            for slot, lhs in ((k, plus), (k - 1, minus)):
                if slot >= 0:
                    first = ns * (a0 - c0) + slot
                    calls.append((ap("pe" + x, S(first, first + ns * st * (cnt - 1) + 1, ns * st)), lhs, rhs))

        if part == 0:
            for k, m, row, span in xt:
                if m and s < 7:
                    add(k, mat("wide", m - 1), mat("wide", m + 3), "x16", row, span)
                else:
                    add(k, mat("base", m), mat("nbase", m), "x16", row, span)
            mm(ap("pe" + x, S(0, ns * w)), eye if s == 7 else mat("diag", 3),
               ap("ce7" if s == 7 else "ce%d" % t, S(0, ns * w)), start=True)
        else:
            for k, m, row, span in ft:
                add(k, mat("base", m), mat("nbase", m), "fl", row, span)
            add(o + 2, mat("diag", 6 if s == 7 else 2), mat("diag", 5 if s == 7 else 1), "fl", 3 * s + 2, vert)
        for i, c in enumerate(calls):
            mm(c[0], c[1], c[2], stop=(s == 7 and part == 1 and i == len(calls) - 1))

    def jumps(tile):
        s, x, c0, c1 = tile
        if s < 7:
            j = 128 * ((s + 1) // 2) + 32 * (1 - s % 2)
            out = ap("pe" + x, S(4, 5 * (c1 - c0), 5))
            mm(out, mat("diag", 3), ap("jb", S(j + c0, j + c1)))
            mm(out, mat("diag", 4), ap("jb", S(j + 64 + c0, j + 64 + c1)), stop=True)

    def gather(tile, k, u0, u1):
        s, x, c0, c1 = tile
        t, fb = s % 2, "fb%d" % (s // 2)
        a0, a1, row, base, sh, dc = c0 + u0, c0 + u1, 0, PAD, 0, 0
        if k == 1:
            row, sh = 1, 1 - 2 * t
        if k == 2:
            dc = -2 if t == 0 else 2
            a0, a1, base = max(a0, -dc), min(a1, 32 - dc), PAD * (2 - 2 * t)
        if k == 3:
            row = 2
        m, o = 16 * (a1 - a0), 16 + 16 * (a0 - c0)
        win = ap(fb, S(base, base + NF))
        off = ap("u16", 3 * s + row, S(a0 + dc, a1 + dc))
        out = ap("d" + x, k, S(o + sh, o + sh + m))
        qq = ap("q", S(16 + 16 * a0 + sh, 16 + 16 * a0 + sh + m))
        op("v", lambda e: e.tensor_tensor(out[0], win[0].indirect(off[0]), qq[0], ALU.subtract), [win, off, qq], [out],
           CALL + LOOKUP * m * CYCLE)
        act(ap("sq%d%s" % (t, x), S(a0 - c0, a1 - c0), S(16 * k, 16 * k + 16)), ap("d" + x, k, S(o, o + m)), ACT.Square)

    def side_parts(tile):
        t, w = tile[0] % 2, tile[3] - tile[2]
        return [(3, min(OPT["side"][t], w)), (2 * t, min(OPT["more"][t], w))]

    def side_bank(tile, m):
        return ap("p7B", S(0, m // 8), S(0, 8)) if tile[1] == "B" and tile[0] < 6 else ap("pg", S(0, m))

    def side_gather(tile, j):
        s, x, c0, c1 = tile
        k, u = side_parts(tile)[j]
        base, row, dc = (0, 0, 2) if k == 2 else (PAD, 2 if k else 0, 0)
        win = ap("fb%d" % (s // 2), S(base, base + NF))
        off = ap("u16", 3 * s + row, S(c0 + dc, c0 + dc + u))
        out = ap("gs", "AB".index(x), S(0, 16 * u))
        op("a", lambda e: e.activation(out[0], win[0].indirect(off[0]), ACT.Identity, bias=0.0, scale=-1.0),
           [win, off], [out], CALL + LOOKUP * 16 * u * CYCLE)

    def side_diff(tile, j):
        s, x, c0, c1 = tile
        m = 16 * side_parts(tile)[j][1]
        mm(side_bank(tile, m), eye, ap("q", S(16 + 16 * c0, 16 + 16 * c0 + m)), start=True)
        mm(side_bank(tile, m), eye, ap("gs", "AB".index(x), S(0, m)), stop=True)

    def side_square(tile, j):
        s, x, c0, c1 = tile
        k, u = side_parts(tile)[j]
        act(ap("sq%d%s" % (s % 2, x), S(0, u), S(16 * k, 16 * k + 16)), side_bank(tile, 16 * u), ACT.Square)

    def least(s, c0, c1):
        return ap("mc", S(NM * s + 5 * c0 + 4, NM * s + 5 * c1, 5))

    def sums_pre(tile):
        s, x, c0, c1 = tile
        w = c1 - c0
        if s == 7:
            mm(ap("p7" + x, S(0, w), S(0, 8)), eye, ap("mask7", S(c0, c1), S(0, 8)), start=True)
            for j, sj in enumerate((1, 3, 5, 6)):
                mm(ap("p7" + x, S(0, w), j), eye, least(sj, c0, c1))
        else:
            mm(ap("ps" + x, S(0, 5 * w)), eye, ap("mask%d" % (s % 2), S(5 * c0, 5 * c1)), start=True)
            if s % 2:
                mm(ap("ps" + x, S(0, 5 * w, 5)), eye, least(s - 1, c0, c1))

    def sums(tile):
        s, x, c0, c1 = tile
        w = c1 - c0
        for r in range(16):
            sel = ap("tsel", S(15 - r, 143 - r))
            if s == 7:
                mm(ap("p7" + x, S(0, w), S(4, 7)), sel, ap("sq1" + x, S(0, w), S(16 + r, 64, 16)), stop=(r == 15))
            else:
                mm(ap("ps" + x, S(0, 5 * w)), sel, ap("sq%d%s" % (s % 2, x), S(0, w), S(r, 80, 16)), stop=(r == 15))

    def pick(tile):
        s, x, c0, c1 = tile
        w, ns = c1 - c0, 8 if s == 7 else 5
        m = ns * w
        mb, mo = ("m7", ns * c0) if s == 7 else ("mc", NM * s + ns * c0)
        ps, ni, z = ap("ps" + x, S(0, m)), ap("ni" + x, S(0, m)), ap("z" + x, S(0, m))

        def one():
            if s == 7:
                cp(ps, ap("p7" + x, S(0, w), S(0, 8)))
            scan(ap(mb, S(mo + 1, mo + 1 + m)), ps, ap("floor7" if s == 7 else "floor", S(0, m)), BIG, ALU.min, ALU.max)

        def two():
            tt(ni, ps, ap(mb, S(mo, mo + m)), ALU.is_ge)
            if s == 7:
                act(ap("oc", S(c0, c1)), ap(mb, S(mo + 7, mo + m, 8)), ACT.Identity, bias=OFF)

        def three():
            u = unit(s, c0 > 0)
            scan(z, ni, ap("pe" + u[1], S(ns * (c0 - u[2]), ns * (c1 - u[2]))), 0.0, ALU.mult, ALU.add)
            if s == 7:
                scan(ap("zf" + x, S(0, m)), ni, ap("dpf", S(0, m)), 0.0, ALU.mult, ALU.add)

        def four():
            if s == 7:
                act(ap("op", S(c0, c1)), ap("z" + x, S(6, m, 8)), ACT.Copy)
                cp(ap("of", S(c0, c1)), ap("zf" + x, S(6, m, 8)))
                return
            v, r = ap("z" + x, S(3, m, 5)), 3 * (s + 1)
            ts(ap("u16", r, S(c0, c1)), v, SHRINK, 0.25 - 0.25 * SHRINK, ALU.mult, ALU.add)
            ts(ap("u16", r + 2, S(c0, c1)), ap("z" + x, S(4, m, 5)), SHRINK, 4095.0, ALU.mult, ALU.min)
            ts(ap("u16", r + 1, S(c0, c1)), v, SHRINK, SIDE[(s + 1) % 2] - 0.25 * SHRINK, ALU.mult, ALU.add)

        return [one, two, three, four]

    nt, per = len(tiles), 3
    for i, tile in enumerate(tiles):
        s, w, j = tile[0], tile[3] - tile[2], i % per
        if i >= per and j in (0, per - 1):
            made = unit(s - 1, j > 0)
            place[0] = i + (OPT["x"][2 * (s % 2) + (j > 0)] if i < nt - 1 else OPT["end"][3])
            task(exact, s, made[2], made[3])
            task(rows_in, s, made[2], made[3])
            task(rows_out, s, made[2], made[3])
        if i == 0:
            task(rows_out, 0, 0, 32)
        if i == 0:
            place[0] = 1.95
            task(second_sweep_constants)
        if i == nt - 2 * per:
            task(act, ap("mask7", S(1, 32, 2), 4), ap("fl", 15, S(0, 16)), ACT.Identity, big15, 0.0)
        aside = dict(side_parts(tile))
        for k, part in enumerate(side_parts(tile)):
            if part[1]:
                task(side_gather, tile, k)
                task(side_diff, tile, k)
                task(side_square, tile, k)
        for turn, k in enumerate(OPT["order"][s % 2] if i % (2 * per) else (1, 0, 2, 3)):
            place[0] = i + (OPT["g"][turn] if i < nt - 1 else OPT["end"][turn])
            if aside.get(k, 0) < w:
                task(gather, tile, k, aside.get(k, 0), w)
        task(sums_pre, tile)
        task(sums, tile)
        if j == 0 or j == per - 1:
            task(steps, unit(s, j > 0), 0)
            task(steps, unit(s, j > 0), 1)
            task(jumps, unit(s, j > 0))
        for late in ([tile] if j == 0 else tiles[i - 1:i + 1] if j == per - 1 else []):
            for turn, f in enumerate(pick(late)):
                place[0] = min(tiles.index(late) + per - 1, nt + OPT["end"][4]) + OPT["p"][turn]
                task(f)
    flush()

    outs = []
    a = ap("oc"); outs.append(dma("s", T.yc[:], a[0], "out0", [a], []))
    a = ap("op"); outs.append(dma("a", T.yp[:], a[0], "out1", [a], []))
    a = ap("of"); outs.append(dma("s", T.yf[:], a[0], "out2", [a], []))
    waits = [("fj%d" % k, nbits(topo.mask(relays_of(T, topo, T.cores[(rank + k) % n])[k], core)), {}) for k in range(1, n)]
    finish("g", [("sent", sent[0], {})] + waits + outs)


def rank_program(g, core, T, topo):
    rank = T.rank_of(core)
    if rank is not None:
        rank_body(g, core, T, topo, rank)
        return
    for src in T.cores:
        rel = relays_of(T, topo, src)
        if core in rel:
            relay_program(g, core, T, topo, src, rel.index(core))
